import numpy as np
import ml_dtypes


def mxq(x, axis, fmt="e4m3"):
    dtype, down = {"e4m3": (ml_dtypes.float8_e4m3fn, 7), "e5m2": (ml_dtypes.float8_e5m2, 14)}[fmt]
    v = np.moveaxis(np.asarray(x, np.float32).astype(ml_dtypes.bfloat16).astype(np.float64), axis, -1)
    blocks = v.reshape(v.shape[:-1] + (-1, 32))
    amax = np.abs(blocks).max(-1, keepdims=True)
    byte = np.maximum(np.where(amax > 0, np.frexp(amax)[1] - 1 + 127, 0) - down, 1)
    scale = np.exp2(byte - 127.0)
    codes = (blocks / scale).astype(np.float32).astype(dtype).astype(np.float64)
    return np.moveaxis((codes * scale).reshape(v.shape), -1, axis)


WIDE = False


def mx_kscale(k):
    if not WIDE:
        return np.ones(k)
    levels = np.array([10, -10, 5, -5, 0])
    if k % 512:
        return np.exp2(np.random.permutation(np.resize(levels, k // 32))).repeat(32)
    a = np.empty((k // 512, 16))
    for p in range(k // 512):
        a[p, :8] = np.random.permutation(np.resize(levels, 8))
        for g in range(8):
            far = levels[np.abs(levels - a[p, g]) >= 10]
            a[p, g + 8] = far[np.random.randint(len(far))]
    return np.exp2(a.ravel()).repeat(32)


BF16 = ml_dtypes.bfloat16


def bf(x):
    return np.asarray(x, np.float32).astype(BF16)


def f64(x):
    return np.asarray(x).astype(np.float64)

def planes(Y):
    n, m = Y.shape
    b = f64(bf(Y)).reshape(n // 32, 32, m)
    amax = np.abs(b).max(1)
    byte = np.clip(np.where(amax > 0, np.frexp(amax)[1] - 1 + 127 - 7, 1), 1, 254)
    codes = (b * np.exp2(127.0 - byte)[:, None, :]).reshape(n, m).astype(np.float32).astype(ml_dtypes.float8_e4m3fn).view(np.uint8)
    words = codes.reshape(n // 512, 128, 4, m).transpose(0, 1, 3, 2)
    return np.ascontiguousarray(words), np.ascontiguousarray(byte.astype(np.uint8).reshape(n // 512, 16, m))


S, D, F = 1024, 512, 2048


def setup_inputs():
    s = mx_kscale(D)
    t = mx_kscale(S)
    x = np.abs(np.random.randn(S, D)) * s[None, :]
    w = np.random.randn(D, F) / np.sqrt(D) / s[:, None]
    gain = (1 + 0.1 * np.random.randn(S)) * t
    a = np.random.randn(S, S) / np.sqrt(S) / t[None, :]
    spread = np.exp(0.8 * np.random.randn(F))
    u = np.random.randn(S)
    b = 0.5 * spread * np.random.randn(F)
    return {"x": bf(x), "w": bf(w), "gain": bf(gain), "a": bf(a),
            "c": bf(spread), "u": bf(u), "b": bf(b)}

def reference(x, w, gain, a, c, u, b):
    x, w, gain, a = f64(x), f64(w), f64(gain), f64(a)
    c, u, b = f64(c), f64(u), f64(b)
    h = mxq(x, 1, "e4m3") @ mxq(w, 0, "e4m3")
    z = np.cos(h) * gain[:, None]
    k = mxq(a, 1, "e4m3") @ mxq(z, 0, "e4m3")
    y = k * c[None, :] + u[:, None] * b[None, :]
    Y = y.T
    words, scales = planes(Y)
    return y, words, scales

@@ -1,0 +1,337 @@
+import math
+from contextlib import ExitStack
+
+import concourse.mybir as mybir
+from concourse.masks import make_identity
+
+S, D, F = 1024, 512, 2048
+FLOPS = 2 * S * D * F + 2 * S * S * F
+
+F32 = mybir.dt.float32
+BF16 = mybir.dt.bfloat16
+I32 = mybir.dt.int32
+U32 = mybir.dt.uint32
+U8 = mybir.dt.uint8
+FP8X4 = mybir.dt.float8_e4m3fn_x4
+ALU = mybir.AluOpType
+ACT = mybir.ActivationFunctionType
+
+P = 128
+GAIN_ON_GPSIMD = True
+KC_LAG = 11
+SUM_LAG = 17
+LAST_SLOT = 64
+TAIL = 33
+A_SLOTS = (3, 4, 5, 6, 7, 8, 9, 10)
+A_Q = (8, 8, 12, 14)
+W_PLAN = ((2, 's', 1, 0, 512), (3, 'g', 2, 0, 512), (9, 's', 3, 0, 256), (12, 's', 3, 256, 512))
+W_Q = (6, 10, 16)
+VEC_SLOT = 8
+CASTS = 'ssssssgvvgggsggs'
+D_ENG = 'gggggggggggggggv'
+TURN_LAG = 2
+UNLOAD_LAG = 0
+QY_LAG = (9, 9, 11, 10, 7, 10, 12, 10)
+LOADS = 'xxwxxwwwagbacw'
+
+
+def tile_network_koopman_step_h3_kernel(tc, x, w, gain, a, c, u, b, out_0, out_1, out_2):
+    nc = tc.nc
+    with ExitStack() as ctx:
+        keep = ctx.enter_context(tc.tile_pool(name="keep", bufs=1))
+        work = ctx.enter_context(tc.tile_pool(name="work", bufs=2))
+        psum = ctx.enter_context(tc.psum_pool(name="psum", bufs=2))
+        ctx.enter_context(tc.manual_schedule())
+
+        def bank(tag):
+            return psum.tile([P, 512], F32, name=tag, tag=tag, bufs={"h": 3, "kt": 2, "tn": 2, "wt": 1}[tag])
+
+        def quantize(codes, scales, src):
+            nc.vector.quantize_mx(out=codes.bitcast(FP8X4), scales=scales, in_=src)
+
+        x_raw = [keep.tile([P, 2, D], BF16, name="x_raw%d" % n) for n in range(4)]
+        w_raw = [keep.tile([P, 4, 512], BF16, name="w_raw%d" % G) for G in range(4)]
+        a_raw = [keep.tile([P, 4, S], BF16, name="a_raw%d" % h) for h in range(2)]
+        gain_sb = keep.tile([P, 2, 4], BF16)
+        rows = keep.tile([P, P], BF16)
+        b_all = keep.tile([P, F], BF16)
+        ident = keep.tile([P, P], F32)
+        warm = keep.tile([P, 1], F32)
+
+        def load_x(n):
+            g, pair = divmod(n, 2)
+            rows_g = x[512 * g : 512 * (g + 1), :].rearrange("(p t) d -> p t d", t=4)
+            nc.sync.dma_start(out=x_raw[n][:], in_=rows_g[:, 2 * pair : 2 * pair + 2, :])
+
+        def load_w(G, lo=0, hi=512):
+            nc.sync.dma_start(out=w_raw[G][:, :, lo:hi], in_=w[:, 512 * G + lo : 512 * G + hi].rearrange("(p j) f -> p j f", j=4))
+
+        def load_a(h):
+            nc.sync.dma_start(out=a_raw[h][:], in_=a[512 * h : 512 * (h + 1), :].rearrange("(s p) k -> p s k", p=P))
+
+        nc.vector.memset(rows[:], 0.0)
+        make_identity(nc, ident[:])
+        nc.scalar.activation(out=warm[:], in_=rows[:, 0:1], func=ACT.Sin)
+        count = {"x": 0, "w": 0, "a": 0}
+        for kind in LOADS:
+            if kind == "x":
+                load_x(count["x"])
+            elif kind == "a":
+                load_a(count["a"])
+            elif kind == "w":
+                load_w(*((0, 0, 256), (0, 256, 512), (1,), (2,), (3,))[count["w"]])
+            elif kind == "g":
+                nc.sync.dma_start(out=gain_sb[:], in_=gain.rearrange("(g p t) -> p g t", g=2, t=4))
+            elif kind == "c":
+                nc.sync.dma_start(out=rows[0:16, :], in_=c.rearrange("(r p) -> r p", p=P))
+                nc.sync.dma_start(out=rows[16:24, :], in_=u.rearrange("(r p) -> r p", p=P))
+            else:
+                nc.sync.dma_start(out=b_all[:], in_=b.partition_broadcast(P))
+            if kind in count:
+                count[kind] += 1
+
+        x_codes = keep.tile([P, 2, 512], U32, align_bytes=64)
+        x_scales = keep.tile([P, 2, 512], U8, align_bytes=64)
+        w_codes = keep.tile([P, F], U32, align_bytes=64)
+        w_scales = keep.tile([P, F], U8, align_bytes=64)
+        a_codes = keep.tile([P, 2, S], U32, align_bytes=64)
+        a_scales = keep.tile([P, 2, S], U8, align_bytes=64)
+        z_codes = keep.tile([P, 16, 256], U32, align_bytes=64)
+        z_scales = keep.tile([P, 16, 256], U8, align_bytes=64)
+        y_scales = keep.tile([P, 4, S], U8, align_bytes=64)
+        rows32 = keep.tile([P, P], F32)
+        cu = keep.tile([P, 32], F32)
+        live = {}
+
+        def turn_words(ps, sources):
+            view = ps[:].rearrange("p (s u m) -> p s u m", s=2, u=2)
+            for s2 in range(2):
+                for uu in range(2):
+                    nc.tensor.transpose(view[:, s2, uu, :], sources(s2, uu), ident[:])
+
+        def unload_words(engine_copy, grouped, pair, ps):
+            dst = grouped[:].bitcast(F32)[:, 512 * pair : 512 * (pair + 1)].rearrange("p (s m u) -> p s m u", s=2, u=2)
+            engine_copy(out=dst, in_=ps[:].rearrange("p (s u m) -> p s m u", s=2, u=2))
+
+        def gpsimd_copy(out, in_):
+            nc.gpsimd.tensor_scalar(out=out, in0=in_, scalar1=1.0, scalar2=1.0, op0=ALU.mult, op1=ALU.mult)
+
+        def interleave_w(engine_copy, G, lo, hi):
+            if lo == 0:
+                live["wg", G] = work.tile([P, 2048], BF16, name="w_grouped", bufs=3, align_bytes=64)
+            dst = live["wg", G][:, 4 * lo : 4 * hi].rearrange("p (f j) -> p f j", j=4)
+            engine_copy(out=dst, in_=w_raw[G][:, :, lo:hi].rearrange("p j f -> p f j"))
+
+        def quantize_w(G, lo, hi):
+            cols = slice(512 * G + lo, 512 * G + hi)
+            quantize(w_codes[:, cols], w_scales[:, cols], live["wg", G][:, 4 * lo : 4 * hi])
+
+        x_grouped = [keep.tile([P, 2048], BF16, name="x_grouped%d" % g, align_bytes=64) for g in range(2)]
+        for n in range(4):
+            ps = bank("tn" if n < 2 else "kt")
+            words = x_raw[n][:].bitcast(F32)
+            turn_words(ps, lambda s2, uu: words[:, s2, uu:256:2])
+            unload_words(nc.scalar.copy, x_grouped[n // 2], n % 2, ps)
+        for g in range(2):
+            interleave_w(nc.vector.tensor_copy, 0, 256 * g, 256 * (g + 1))
+            quantize(x_codes[:, g, :], x_scales[:, g, :], x_grouped[g][:])
+            quantize_w(0, 256 * g, 256 * (g + 1))
+
+        def lift(n):
+            ft, g = divmod(n, 2)
+            ps = bank("h")
+            live["h", n] = ps
+            for t in range(4):
+                xc = slice(128 * t, 128 * (t + 1))
+                wc = slice(128 * ft, 128 * (ft + 1))
+                nc.tensor.matmul_mx(
+                    out=ps[:, xc], lhsT=x_codes[:, g, xc].bitcast(FP8X4), lhsT_scale=x_scales[:, g, xc],
+                    rhs=w_codes[:, wc].bitcast(FP8X4), rhs_scale=w_scales[:, wc], start=True, stop=True)
+
+        def h_view(n):
+            return live["h", n][:].rearrange("p (t f) -> p f t", t=4)
+
+        def count_turns(n):
+            turns = work.tile([P, P, 4], I32, name="turns", bufs=3)
+            live["turns", n] = turns
+            nc.vector.tensor_scalar(out=turns[:], in0=h_view(n), scalar1=1.0 / (2.0 * math.pi), scalar2=0.25,
+                                    op0=ALU.mult, op1=ALU.add)
+
+        def reduce_angle(n):
+            if n % 2 == 0:
+                live["angle", n // 2] = work.tile([P, 2, P, 4], F32, name="angle", bufs=2)
+            angle = live["angle", n // 2]
+            nc.vector.scalar_tensor_tensor(out=angle[:, n % 2], in0=live["turns", n][:], scalar=-2.0 * math.pi, in1=h_view(n),
+                                           op0=ALU.mult, op1=ALU.add)
+
+        def cosine(ft):
+            live["cos", ft] = work.tile([P, 2, P, 4], F32, name="cos", bufs=2)
+            nc.scalar.activation(out=live["cos", ft][:].rearrange("p g f t -> p (g f t)"),
+                                 in_=live["angle", ft][:].rearrange("p g f t -> p (g f t)"), func=ACT.Sin, bias=math.pi / 2.0)
+
+        def apply_gain(ft):
+            z = work.tile([P, 2, P, 4], BF16, name="z", bufs=1, align_bytes=64)
+            live["z", ft] = z
+            engine = nc.gpsimd if D_ENG[ft] == "g" else nc.vector
+            engine.tensor_tensor(out=z[:], in0=live["cos", ft][:], in1=gain_sb[:].unsqueeze(2).to_broadcast([P, 2, P, 4]),
+                                 op=ALU.mult)
+
+        def quantize_z(ft):
+            quantize(z_codes[:, ft, :], z_scales[:, ft, :], live["z", ft][:].rearrange("p g f t -> p (g f t)"))
+
+        def couple(m):
+            ft, h = 4 * (m // 8) + m % 4, (m // 4) % 2
+            ps = bank("kt")
+            live["kt", m] = ps
+            for g in range(2):
+                zc = slice(128 * g, 128 * (g + 1))
+                ac = slice(512 * h, 512 * (h + 1))
+                nc.tensor.matmul_mx(
+                    out=ps[:], lhsT=z_codes[:, ft, zc].bitcast(FP8X4), lhsT_scale=z_scales[:, ft, zc],
+                    rhs=a_codes[:, g, ac].bitcast(FP8X4), rhs_scale=a_scales[:, g, ac], start=(g == 0), stop=(g == 1))
+
+        def scale_c(m):
+            j, q = divmod(m, 4)
+            ft = 4 * (j // 2) + q
+            if q == 0:
+                live["kc", j] = work.tile([P, 4, 512], F32, name="kc", bufs=3)
+            nc.scalar.activation(out=live["kc", j][:, q, :], in_=live["kt", m][:], func=ACT.Copy, scale=cu[:, ft : ft + 1])
+
+        def turn_kc(j, s, tag):
+            ps = bank(tag)
+            live["tn", j, s] = ps
+            for q in range(4):
+                nc.tensor.transpose(ps[:, 128 * q : 128 * (q + 1)], live["kc", j][:, q, 128 * s : 128 * (s + 1)], ident[:])
+
+        def add_control(j, s):
+            G, h = divmod(j, 2)
+            if s % 2 == 0:
+                live["y", j, s // 2] = work.tile([P, 2, 512], F32, name="y", bufs=4)
+            y = live["y", j, s // 2]
+            col = 16 + 4 * h + s
+            nc.vector.scalar_tensor_tensor(out=y[:, s % 2, :], in0=b_all[:, 512 * G : 512 * (G + 1)], scalar=cu[:, col : col + 1],
+                                           in1=live["tn", j, s][:], op0=ALU.mult, op1=ALU.add)
+            if s % 2 == 1:
+                r0 = 512 * h + 128 * (s - 1)
+                nc.sync.dma_start(out=out_0[r0 : r0 + 256, 512 * G : 512 * (G + 1)].rearrange("(s p) f -> p s f", p=P), in_=y[:])
+
+        def round_y(engine, j, pair):
+            yb = work.tile([P, 1024], BF16, name="y_bf16", bufs=3)
+            live["yb", j, pair] = yb
+            dst = yb[:].rearrange("p (u q e) -> p u q e", u=2, e=2)
+            src = live["y", j, pair][:].rearrange("p s (q u e) -> p u (s q) e", u=2, e=2)
+            if engine == "gpsimd":
+                gpsimd_copy(dst, src)
+            elif engine == "scalar":
+                nc.scalar.copy(out=dst, in_=src)
+            else:
+                nc.vector.tensor_copy(out=dst, in_=src)
+
+        def turn_y(j, pair, tag):
+            ps = bank(tag)
+            live["wt", j, pair] = ps
+            words = live["yb", j, pair][:].bitcast(F32)
+            turn_words(ps, lambda s2, uu: words[:, 256 * uu + 128 * s2 : 256 * uu + 128 * (s2 + 1)])
+
+        def unload_y(j, pair):
+            if pair == 0:
+                live["yg", j] = work.tile([P, 2048], BF16, name="y_grouped", align_bytes=64)
+            unload_words(nc.scalar.copy, live["yg", j], pair, live["wt", j, pair])
+
+        def quantize_y(j):
+            G, h = divmod(j, 2)
+            codes = work.tile([P, 512], U32, name="y_codes", align_bytes=64)
+            cols = slice(512 * h, 512 * (h + 1))
+            quantize(codes[:], y_scales[:, G, cols], live["yg", j][:])
+            nc.sync.dma_start(out=out_1[G, :, cols, :].rearrange("p m t -> p (m t)").bitcast(I32), in_=codes[:].bitcast(I32))
+            if h == 1:
+                for Q in range(4):
+                    nc.sync.dma_start(out=out_2[G, 4 * Q : 4 * Q + 4, :].bitcast(I32),
+                                      in_=y_scales[32 * Q : 32 * Q + 4, G, :].bitcast(I32))
+
+        def turn_a(n):
+            h, g, pair = n // 4, (n // 2) % 2, n % 2
+            ps = bank("tn")
+            live["at", n] = ps
+            words = a_raw[h][:].bitcast(F32)
+            turn_words(ps, lambda s2, uu: words[:, 2 * pair + s2, 256 * g + uu : 256 * (g + 1) : 2])
+
+        def unload_a(n):
+            if n % 2 == 0:
+                live["ag", n // 2] = work.tile([P, 2048], BF16, name="a_grouped", align_bytes=64)
+            unload_words(nc.scalar.copy, live["ag", n // 2], n % 2, live["at", n])
+
+        def quantize_a(m):
+            h, g = divmod(m, 2)
+            cols = slice(512 * h, 512 * (h + 1))
+            quantize(a_codes[:, g, cols], a_scales[:, g, cols], live["ag", m][:])
+
+        def small_vectors():
+            nc.scalar.copy(out=rows32[:], in_=rows[:])
+            ps = bank("wt")
+            nc.tensor.transpose(ps[:, 0:P], rows32[:], ident[:])
+            nc.scalar.copy(out=cu[:], in_=ps[:, 0:32])
+
+        def due(slot, lag, count):
+            n = slot - lag
+            return [n] if 0 <= n < count else []
+
+        lift(0)
+        for slot in range(LAST_SLOT):
+            casts = [({"g": "gpsimd", "s": "scalar", "v": "vector"}[CASTS[n // 2]], n // 4, (n % 4) // 2) for n in due(slot, SUM_LAG + 1, 32) if n % 2 == 1]
+            for j in range(8):
+                if slot == SUM_LAG + 4 * j + QY_LAG[j]:
+                    quantize_y(j)
+            for when, engine, G, lo, hi in W_PLAN:
+                if slot == when and engine != "s":
+                    interleave_w(nc.vector.tensor_copy if engine == "v" else gpsimd_copy, G, lo, hi)
+            if slot in W_Q:
+                quantize_w(1 + W_Q.index(slot), 0, 512)
+            for m in range(4):
+                if slot == A_Q[m]:
+                    quantize_a(m)
+            if slot == VEC_SLOT:
+                small_vectors()
+            if slot % 2 == 0:
+                for n in due(slot, 6, 32):
+                    quantize_z(n // 2)
+                for n in due(slot, 4, 32):
+                    apply_gain(n // 2)
+            for engine, j, pair in casts:
+                if engine == "gpsimd":
+                    round_y(engine, j, pair)
+            for n in range(8):
+                if slot == A_SLOTS[n]:
+                    turn_a(n)
+            for n in due(slot, SUM_LAG - 1, 32):
+                turn_kc(n // 4, n % 4, "tn" if slot < TAIL or n % 2 == 0 else "h")
+            for n in due(slot, SUM_LAG + 1 + TURN_LAG, 32):
+                if n % 2 == 1:
+                    turn_y(n // 4, (n % 4) // 2, "wt" if slot < KC_LAG + 33 or n % 4 == 1 else "kt")
+            for n in due(slot, -1, 32):
+                lift(n)
+            for n in due(slot, KC_LAG - 1, 32):
+                couple(n)
+            for n in due(slot, 0, 32):
+                count_turns(n)
+            for n in due(slot, SUM_LAG, 32):
+                add_control(n // 4, n % 4)
+            for n in due(slot, 1, 32):
+                reduce_angle(n)
+            for n in due(slot, 2, 32):
+                if n % 2 == 1:
+                    cosine(n // 2)
+            for engine, j, pair in casts:
+                if engine != "gpsimd":
+                    round_y(engine, j, pair)
+            for n in due(slot, KC_LAG, 32):
+                scale_c(n)
+            for n in due(slot, SUM_LAG + 1 + TURN_LAG + UNLOAD_LAG, 32):
+                if n % 2 == 1:
+                    unload_y(n // 4, (n % 4) // 2)
+            for n in range(8):
+                if slot == A_SLOTS[n] + 1:
+                    unload_a(n)
+            for when, engine, G, lo, hi in W_PLAN:
+                if slot == when and engine == "s":
+                    interleave_w(nc.scalar.copy, G, lo, hi)

@@ -18,21 +18,26 @@ ACT = mybir.ActivationFunctionType
 
 P = 128
 GAIN_ON_GPSIMD = True
-KC_LAG = 11
-SUM_LAG = 17
+KC_LAG = 9
+SUM_LAG = 16
 LAST_SLOT = 64
-TAIL = 33
-A_SLOTS = (3, 4, 5, 6, 7, 8, 9, 10)
-A_Q = (8, 8, 12, 14)
-W_PLAN = ((2, 's', 1, 0, 512), (3, 'g', 2, 0, 512), (9, 's', 3, 0, 256), (12, 's', 3, 256, 512))
-W_Q = (6, 10, 16)
+X_FIRST = 3
+LAST_LAG = 8
+TAIL = 34
+A_SLOTS = (3, 4, 5, 5, 5, 6, 7, 8)
+A_Q = (6, 8, 10, 10)
+W_PLAN = ((3, 's', 1, 0, 256, 6), (5, 's', 1, 256, 512, 10), (8, 's', 2, 0, 256, 10), (14, 's', 2, 256, 512, 18), (16, 'g', 3, 0, 128, 22), (16, 'v', 3, 128, 256, 24), (19, 's', 3, 256, 384, 24), (19, 'g', 3, 384, 512, 22))
+WARM = '2111221002030030330303000301030300010000000300000000031203200102'
+UNLOAD_ENG = 'ssssssvsssssssvs'
+A_ENG = 'ssssvsvs'
+KC_ENG = 'ssvsssvssssssssssssssssssvvssvss'
 VEC_SLOT = 8
-CASTS = 'ssssssgvvgggsggs'
-D_ENG = 'gggggggggggggggv'
+CASTS = 'ssssssssssvssvsg'
+D_ENG = 'gggggggggggggggg'
 TURN_LAG = 2
 UNLOAD_LAG = 0
-QY_LAG = (9, 9, 11, 10, 7, 10, 12, 10)
-LOADS = 'xxwxxwwwagbacw'
+QY_LAG = (8, 10, 10, 10, 9, 10, 8, 12, 18)
+LOADS = 'xxwxgxwwaacwbw'
 
 
 def tile_network_koopman_step_h3_kernel(tc, x, w, gain, a, c, u, b, out_0, out_1, out_2):
@@ -96,8 +101,8 @@ def tile_network_koopman_step_h3_kernel(tc, x, w, gain, a, c, u, b, out_0, out_1
         w_scales = keep.tile([P, F], U8, align_bytes=64)
         a_codes = keep.tile([P, 2, S], U32, align_bytes=64)
         a_scales = keep.tile([P, 2, S], U8, align_bytes=64)
-        z_codes = keep.tile([P, 16, 256], U32, align_bytes=64)
-        z_scales = keep.tile([P, 16, 256], U8, align_bytes=64)
+        z_codes = keep.tile([P, 32 * P], U32, align_bytes=64)
+        z_scales = keep.tile([P, 32 * P], U8, align_bytes=64)
         y_scales = keep.tile([P, 4, S], U8, align_bytes=64)
         rows32 = keep.tile([P, P], F32)
         cu = keep.tile([P, 32], F32)
@@ -116,29 +121,44 @@ def tile_network_koopman_step_h3_kernel(tc, x, w, gain, a, c, u, b, out_0, out_1
         def gpsimd_copy(out, in_):
             nc.gpsimd.tensor_scalar(out=out, in0=in_, scalar1=1.0, scalar2=1.0, op0=ALU.mult, op1=ALU.mult)
 
-        def interleave_w(engine_copy, G, lo, hi):
-            if lo == 0:
-                live["wg", G] = work.tile([P, 2048], BF16, name="w_grouped", bufs=3, align_bytes=64)
-            dst = live["wg", G][:, 4 * lo : 4 * hi].rearrange("p (f j) -> p f j", j=4)
-            engine_copy(out=dst, in_=w_raw[G][:, :, lo:hi].rearrange("p j f -> p f j"))
+        def interleave_w(engine, G, lo, hi):
+            if engine == "g":
+                grouped = work.tile([P, 4 * (hi - lo)], BF16, name="w_grouped_g", bufs=2, align_bytes=64)
+            else:
+                grouped = work.tile([P, 4 * (hi - lo)], BF16, name="w_grouped", bufs=2, align_bytes=64)
+            live["wg", G, lo] = grouped
+            copies[engine](out=grouped[:].rearrange("p (f j) -> p f j", j=4), in_=w_raw[G][:, :, lo:hi].rearrange("p j f -> p f j"))
 
         def quantize_w(G, lo, hi):
             cols = slice(512 * G + lo, 512 * G + hi)
-            quantize(w_codes[:, cols], w_scales[:, cols], live["wg", G][:, 4 * lo : 4 * hi])
+            quantize(w_codes[:, cols], w_scales[:, cols], live["wg", G, lo][:])
 
-        x_grouped = [keep.tile([P, 2048], BF16, name="x_grouped%d" % g, align_bytes=64) for g in range(2)]
-        for n in range(4):
+        copies = {"g": gpsimd_copy, "s": nc.scalar.copy, "v": nc.vector.tensor_copy}
+
+        x_grouped = [keep.tile([P, 2048], BF16, name="x_grouped0", align_bytes=64),
+                     keep.tile([P, 2048], BF16, name="x_grouped1", align_bytes=64)]
+
+        def turn_x(n):
             ps = bank("tn" if n < 2 else "kt")
             words = x_raw[n][:].bitcast(F32)
             turn_words(ps, lambda s2, uu: words[:, s2, uu:256:2])
             unload_words(nc.scalar.copy, x_grouped[n // 2], n % 2, ps)
-        for g in range(2):
-            interleave_w(nc.vector.tensor_copy, 0, 256 * g, 256 * (g + 1))
-            quantize(x_codes[:, g, :], x_scales[:, g, :], x_grouped[g][:])
-            quantize_w(0, 256 * g, 256 * (g + 1))
+
+        for n in range(X_FIRST):
+            turn_x(n)
+        interleave_w("v", 0, 0, 256)
+        quantize(x_codes[:, 0, 0:256], x_scales[:, 0, 0:256], x_grouped[0][:, 0:1024])
+        quantize_w(0, 0, 256)
+        quantize(x_codes[:, 0, 256:512], x_scales[:, 0, 256:512], x_grouped[0][:, 1024:2048])
+
+        def warm_up(count):
+            ps = bank("wt" if count < 0 else "wt")
+            for i in range(count):
+                nc.tensor.matmul_mx(out=ps[:], lhsT=w_codes[:, 0:P].bitcast(FP8X4), lhsT_scale=w_scales[:, 0:P],
+                                    rhs=x_codes[:, 0, :].bitcast(FP8X4), rhs_scale=x_scales[:, 0, :], start=True, stop=True)
 
         def lift(n):
-            ft, g = divmod(n, 2)
+            ft, g = lifting(n)
             ps = bank("h")
             live["h", n] = ps
             for t in range(4):
@@ -170,32 +190,46 @@ def tile_network_koopman_step_h3_kernel(tc, x, w, gain, a, c, u, b, out_0, out_1
                                  in_=live["angle", ft][:].rearrange("p g f t -> p (g f t)"), func=ACT.Sin, bias=math.pi / 2.0)
 
         def apply_gain(ft):
-            z = work.tile([P, 2, P, 4], BF16, name="z", bufs=1, align_bytes=64)
+            z = work.tile([P, 2, P, 4], BF16, name="z", tag="z", bufs=1, align_bytes=64)
             live["z", ft] = z
+            gains = gain_sb[:, ft : ft + 1, :] if ft < 2 else gain_sb[:]
             engine = nc.gpsimd if D_ENG[ft] == "g" else nc.vector
-            engine.tensor_tensor(out=z[:], in0=live["cos", ft][:], in1=gain_sb[:].unsqueeze(2).to_broadcast([P, 2, P, 4]),
+            engine.tensor_tensor(out=z[:], in0=live["cos", ft][:], in1=gains.unsqueeze(2).to_broadcast([P, 2, P, 4]),
                                  op=ALU.mult)
 
         def quantize_z(ft):
-            quantize(z_codes[:, ft, :], z_scales[:, ft, :], live["z", ft][:].rearrange("p g f t -> p (g f t)"))
+            quantize(z_codes[:, 256 * ft : 256 * (ft + 1)], z_scales[:, 256 * ft : 256 * (ft + 1)], live["z", ft][:].rearrange("p g f t -> p (g f t)"))
+
+        def coupling(m):
+            q, h = ((0, 0), (1, 0), (2, 0), (0, 1), (3, 0), (1, 1), (2, 1), (3, 1))[m % 8]
+            return 4 * (m // 8) + q, h
+
+        def lifting(n):
+            return (n % 2, n // 2) if n < 4 else divmod(n, 2)
+
+        def z_block(ft, g):
+            return 2 * g + ft if ft < 2 else 2 * ft + g
 
         def couple(m):
-            ft, h = 4 * (m // 8) + m % 4, (m // 4) % 2
+            ft, h = coupling(m)
             ps = bank("kt")
             live["kt", m] = ps
             for g in range(2):
-                zc = slice(128 * g, 128 * (g + 1))
+                zc = slice(P * z_block(ft, g), P * (z_block(ft, g) + 1))
                 ac = slice(512 * h, 512 * (h + 1))
                 nc.tensor.matmul_mx(
-                    out=ps[:], lhsT=z_codes[:, ft, zc].bitcast(FP8X4), lhsT_scale=z_scales[:, ft, zc],
+                    out=ps[:], lhsT=z_codes[:, zc].bitcast(FP8X4), lhsT_scale=z_scales[:, zc],
                     rhs=a_codes[:, g, ac].bitcast(FP8X4), rhs_scale=a_scales[:, g, ac], start=(g == 0), stop=(g == 1))
 
         def scale_c(m):
-            j, q = divmod(m, 4)
-            ft = 4 * (j // 2) + q
+            ft, h = coupling(m)
+            j, q = 2 * (ft // 4) + h, ft % 4
             if q == 0:
-                live["kc", j] = work.tile([P, 4, 512], F32, name="kc", bufs=3)
-            nc.scalar.activation(out=live["kc", j][:, q, :], in_=live["kt", m][:], func=ACT.Copy, scale=cu[:, ft : ft + 1])
+                live["kc", j] = work.tile([P, 4, 512], F32, name="kc", bufs=4)
+            if KC_ENG[m] == "s":
+                nc.scalar.activation(out=live["kc", j][:, q, :], in_=live["kt", m][:], func=ACT.Copy, scale=cu[:, ft : ft + 1])
+            else:
+                nc.vector.tensor_scalar(out=live["kc", j][:, q, :], in0=live["kt", m][:], scalar1=cu[:, ft : ft + 1], scalar2=None, op0=ALU.mult)
 
         def turn_kc(j, s, tag):
             ps = bank(tag)
@@ -236,22 +270,38 @@ def tile_network_koopman_step_h3_kernel(tc, x, w, gain, a, c, u, b, out_0, out_1
         def unload_y(j, pair):
             if pair == 0:
                 live["yg", j] = work.tile([P, 2048], BF16, name="y_grouped", align_bytes=64)
-            unload_words(nc.scalar.copy, live["yg", j], pair, live["wt", j, pair])
+            unload_words(copies[UNLOAD_ENG[2 * j + pair]], live["yg", j], pair, live["wt", j, pair])
 
-        def quantize_y(j):
+        def finish_last():
+            for s in (2, 3):
+                yb = work.tile([P, 512], BF16, name="y_bf16_last")
+                live["last", s] = yb
+                copies["s" if s == 2 else "v"](out=yb[:].rearrange("p (u q e) -> p u q e", u=2, e=2),
+                                               in_=live["y", 7, 1][:, s % 2, :].rearrange("p (q u e) -> p u q e", u=2, e=2))
+            for s in (2, 3):
+                ps = bank("kt")
+                live["last_ps", s] = ps
+                for uu in range(2):
+                    nc.tensor.transpose(ps[:, P * uu : P * (uu + 1)], live["last", s][:].bitcast(F32)[:, P * uu : P * (uu + 1)], ident[:])
+            for s in (2, 3):
+                dst = live["yg", 7][:].bitcast(F32)[:, 256 * s : 256 * (s + 1)].rearrange("p (m u) -> p m u", u=2)
+                copies["s" if s == 2 else "v"](out=dst, in_=live["last_ps", s][:, 0:256].rearrange("p (u m) -> p m u", u=2))
+
+        def quantize_y(j, lo, hi):
             G, h = divmod(j, 2)
-            codes = work.tile([P, 512], U32, name="y_codes", align_bytes=64)
-            cols = slice(512 * h, 512 * (h + 1))
-            quantize(codes[:], y_scales[:, G, cols], live["yg", j][:])
+            codes = work.tile([P, hi - lo], U32, name="y_codes", bufs=3, align_bytes=64)
+            cols = slice(512 * h + lo, 512 * h + hi)
+            quantize(codes[:], y_scales[:, G, cols], live["yg", j][:, 4 * lo : 4 * hi])
             nc.sync.dma_start(out=out_1[G, :, cols, :].rearrange("p m t -> p (m t)").bitcast(I32), in_=codes[:].bitcast(I32))
-            if h == 1:
+            if h == 1 and hi == 512:
                 for Q in range(4):
-                    nc.sync.dma_start(out=out_2[G, 4 * Q : 4 * Q + 4, :].bitcast(I32),
-                                      in_=y_scales[32 * Q : 32 * Q + 4, G, :].bitcast(I32))
+                    queue = nc.scalar if j == 7 and Q % 2 == 1 else nc.sync
+                    queue.dma_start(out=out_2[G, 4 * Q : 4 * Q + 4, :].bitcast(I32),
+                                    in_=y_scales[32 * Q : 32 * Q + 4, G, :].bitcast(I32))
 
         def turn_a(n):
             h, g, pair = n // 4, (n // 2) % 2, n % 2
-            ps = bank("tn")
+            ps = bank("kt" if n > 0 and A_SLOTS[n] == A_SLOTS[n - 1] else "tn")
             live["at", n] = ps
             words = a_raw[h][:].bitcast(F32)
             turn_words(ps, lambda s2, uu: words[:, 2 * pair + s2, 256 * g + uu : 256 * (g + 1) : 2])
@@ -259,7 +309,7 @@ def tile_network_koopman_step_h3_kernel(tc, x, w, gain, a, c, u, b, out_0, out_1
         def unload_a(n):
             if n % 2 == 0:
                 live["ag", n // 2] = work.tile([P, 2048], BF16, name="a_grouped", align_bytes=64)
-            unload_words(nc.scalar.copy, live["ag", n // 2], n % 2, live["at", n])
+            unload_words(copies[A_ENG[n]], live["ag", n // 2], n % 2, live["at", n])
 
         def quantize_a(m):
             h, g = divmod(m, 2)
@@ -277,16 +327,29 @@ def tile_network_koopman_step_h3_kernel(tc, x, w, gain, a, c, u, b, out_0, out_1
             return [n] if 0 <= n < count else []
 
         lift(0)
-        for slot in range(LAST_SLOT):
-            casts = [({"g": "gpsimd", "s": "scalar", "v": "vector"}[CASTS[n // 2]], n // 4, (n % 4) // 2) for n in due(slot, SUM_LAG + 1, 32) if n % 2 == 1]
-            for j in range(8):
+        lift(1)
+        for n in range(X_FIRST, 4):
+            turn_x(n)
+        warm_up(int(WARM[0]))
+        interleave_w("v", 0, 256, 512)
+        count_turns(0)
+        count_turns(1)
+        reduce_angle(0)
+        quantize(x_codes[:, 1, :], x_scales[:, 1, :], x_grouped[1][:])
+        lift(2)
+        for slot in range(2, LAST_SLOT):
+            casts = [({"g": "gpsimd", "s": "scalar", "v": "vector"}[CASTS[n // 2]], n // 4, (n % 4) // 2) for n in due(slot, SUM_LAG + 1, 31) if n % 2 == 1]
+            for j in range(7):
                 if slot == SUM_LAG + 4 * j + QY_LAG[j]:
-                    quantize_y(j)
-            for when, engine, G, lo, hi in W_PLAN:
-                if slot == when and engine != "s":
-                    interleave_w(nc.vector.tensor_copy if engine == "v" else gpsimd_copy, G, lo, hi)
-            if slot in W_Q:
-                quantize_w(1 + W_Q.index(slot), 0, 512)
+                    quantize_y(j, 0, 512)
+            for pair in range(2):
+                if slot == SUM_LAG + 28 + QY_LAG[7 + pair]:
+                    quantize_y(7, 256 * pair, 256 * (pair + 1))
+            for when, engine, G, lo, hi, when_q in W_PLAN:
+                if slot == when and engine == "v":
+                    interleave_w(engine, G, lo, hi)
+                if slot == when_q:
+                    quantize_w(G, lo, hi)
             for m in range(4):
                 if slot == A_Q[m]:
                     quantize_a(m)
@@ -295,8 +358,12 @@ def tile_network_koopman_step_h3_kernel(tc, x, w, gain, a, c, u, b, out_0, out_1
             if slot % 2 == 0:
                 for n in due(slot, 6, 32):
                     quantize_z(n // 2)
+            if slot % 2 == 0:
                 for n in due(slot, 4, 32):
                     apply_gain(n // 2)
+            for when, engine, G, lo, hi, when_q in W_PLAN:
+                if slot == when and engine == "g":
+                    interleave_w(engine, G, lo, hi)
             for engine, j, pair in casts:
                 if engine == "gpsimd":
                     round_y(engine, j, pair)
@@ -305,19 +372,26 @@ def tile_network_koopman_step_h3_kernel(tc, x, w, gain, a, c, u, b, out_0, out_1
                     turn_a(n)
             for n in due(slot, SUM_LAG - 1, 32):
                 turn_kc(n // 4, n % 4, "tn" if slot < TAIL or n % 2 == 0 else "h")
-            for n in due(slot, SUM_LAG + 1 + TURN_LAG, 32):
+            for n in due(slot, SUM_LAG + 1 + TURN_LAG, 31):
                 if n % 2 == 1:
                     turn_y(n // 4, (n % 4) // 2, "wt" if slot < KC_LAG + 33 or n % 4 == 1 else "kt")
             for n in due(slot, -1, 32):
-                lift(n)
+                if n > 1:
+                    lift(n)
             for n in due(slot, KC_LAG - 1, 32):
                 couple(n)
+            if WARM[slot] != "0":
+                warm_up(int(WARM[slot]))
+            if slot == 2:
+                reduce_angle(1)
+                quantize_w(0, 256, 512)
             for n in due(slot, 0, 32):
                 count_turns(n)
             for n in due(slot, SUM_LAG, 32):
                 add_control(n // 4, n % 4)
             for n in due(slot, 1, 32):
-                reduce_angle(n)
+                if n > 1:
+                    reduce_angle(n)
             for n in due(slot, 2, 32):
                 if n % 2 == 1:
                     cosine(n // 2)
@@ -326,12 +400,14 @@ def tile_network_koopman_step_h3_kernel(tc, x, w, gain, a, c, u, b, out_0, out_1
                     round_y(engine, j, pair)
             for n in due(slot, KC_LAG, 32):
                 scale_c(n)
-            for n in due(slot, SUM_LAG + 1 + TURN_LAG + UNLOAD_LAG, 32):
+            for n in due(slot, SUM_LAG + 1 + TURN_LAG + UNLOAD_LAG, 31):
                 if n % 2 == 1:
                     unload_y(n // 4, (n % 4) // 2)
+            if slot == SUM_LAG + 28 + LAST_LAG:
+                finish_last()
             for n in range(8):
                 if slot == A_SLOTS[n] + 1:
                     unload_a(n)
-            for when, engine, G, lo, hi in W_PLAN:
+            for when, engine, G, lo, hi, when_q in W_PLAN:
                 if slot == when and engine == "s":
-                    interleave_w(nc.scalar.copy, G, lo, hi)
+                    interleave_w(engine, G, lo, hi)

@@ -22,22 +22,22 @@ KC_LAG = 9
 SUM_LAG = 16
 LAST_SLOT = 64
 X_FIRST = 3
-LAST_LAG = 8
-TAIL = 34
-A_SLOTS = (3, 4, 5, 5, 5, 6, 7, 8)
-A_Q = (6, 8, 10, 10)
-W_PLAN = ((3, 's', 1, 0, 256, 6), (5, 's', 1, 256, 512, 10), (8, 's', 2, 0, 256, 10), (14, 's', 2, 256, 512, 18), (16, 'g', 3, 0, 128, 22), (16, 'v', 3, 128, 256, 24), (19, 's', 3, 256, 384, 24), (19, 'g', 3, 384, 512, 22))
-WARM = '2111221002030030330303000301030300010000000300000000031203200102'
-UNLOAD_ENG = 'ssssssvsssssssvs'
-A_ENG = 'ssssvsvs'
-KC_ENG = 'ssvsssvssssssssssssssssssvvssvss'
-VEC_SLOT = 8
-CASTS = 'ssssssssssvssvsg'
-D_ENG = 'gggggggggggggggg'
+LAST_LAG = 4
+LAST_GAP = 2
+TAIL = 33
+A_SLOTS = (2, 3, 4, 4, 5, 7, 7, 8)
+A_Q = (5, 8, 10, 10)
+W_PLAN = ((3, 's', 1, 0, 256, 5), (6, 's', 1, 256, 512, 10), (9, 's', 2, 0, 256, 12), (11, 's', 2, 256, 512, 14), (14, 's', 3, 0, 256, 16), (15, 's', 3, 256, 512, 24))
+UNLOAD_ENG = 'ssssssvssssssssv'
+A_ENG = 'ssssssss'
+KC_ENG = 'ssssssssssssssssssssssssssssssss'
+VEC_SLOT = 6
+CASTS = 'hhsshsssvghhhgss'
+D_ENG = 'gggggggggggggggv'
 TURN_LAG = 2
 UNLOAD_LAG = 0
-QY_LAG = (8, 10, 10, 10, 9, 10, 8, 12, 18)
-LOADS = 'xxwxgxwwaacwbw'
+QY_LAG = (12, 12, 10, 10, 9, 11, 8, 6, 9)
+LOADS = 'gxxwxwxawacwbw'
 
 
 def tile_network_koopman_step_h3_kernel(tc, x, w, gain, a, c, u, b, out_0, out_1, out_2):
@@ -95,6 +95,12 @@ def tile_network_koopman_step_h3_kernel(tc, x, w, gain, a, c, u, b, out_0, out_1
             if kind in count:
                 count[kind] += 1
 
+        gain_all = keep.tile([P, 2, 1024], F32)
+
+        def spread_gain(g):
+            nc.scalar.copy(out=gain_all[:, g, :].rearrange("p (f t) -> p f t", t=4), in_=gain_sb[:, g : g + 1, :].to_broadcast([P, 256, 4]))
+
+        spread_gain(0)
         x_codes = keep.tile([P, 2, 512], U32, align_bytes=64)
         x_scales = keep.tile([P, 2, 512], U8, align_bytes=64)
         w_codes = keep.tile([P, F], U32, align_bytes=64)
@@ -146,76 +152,66 @@ def tile_network_koopman_step_h3_kernel(tc, x, w, gain, a, c, u, b, out_0, out_1
 
         for n in range(X_FIRST):
             turn_x(n)
-        interleave_w("v", 0, 0, 256)
-        quantize(x_codes[:, 0, 0:256], x_scales[:, 0, 0:256], x_grouped[0][:, 0:1024])
-        quantize_w(0, 0, 256)
-        quantize(x_codes[:, 0, 256:512], x_scales[:, 0, 256:512], x_grouped[0][:, 1024:2048])
 
-        def warm_up(count):
-            ps = bank("wt" if count < 0 else "wt")
-            for i in range(count):
-                nc.tensor.matmul_mx(out=ps[:], lhsT=w_codes[:, 0:P].bitcast(FP8X4), lhsT_scale=w_scales[:, 0:P],
-                                    rhs=x_codes[:, 0, :].bitcast(FP8X4), rhs_scale=x_scales[:, 0, :], start=True, stop=True)
+        def quantize_x(n):
+            g, cols = n // 2, slice(256 * (n % 2), 256 * (n % 2 + 1))
+            quantize(x_codes[:, g, cols], x_scales[:, g, cols], x_grouped[g][:, 1024 * (n % 2) : 1024 * (n % 2 + 1)])
 
         def lift(n):
-            ft, g = lifting(n)
+            fh, g, pair = n // 4, (n // 2) % 2, n % 2
             ps = bank("h")
             live["h", n] = ps
-            for t in range(4):
-                xc = slice(128 * t, 128 * (t + 1))
-                wc = slice(128 * ft, 128 * (ft + 1))
+            wc = slice(256 * fh, 256 * (fh + 1))
+            for e in range(2):
+                xc = slice(P * (2 * pair + e), P * (2 * pair + e + 1))
                 nc.tensor.matmul_mx(
-                    out=ps[:, xc], lhsT=x_codes[:, g, xc].bitcast(FP8X4), lhsT_scale=x_scales[:, g, xc],
+                    out=ps[:, 256 * e : 256 * (e + 1)], lhsT=x_codes[:, g, xc].bitcast(FP8X4), lhsT_scale=x_scales[:, g, xc],
                     rhs=w_codes[:, wc].bitcast(FP8X4), rhs_scale=w_scales[:, wc], start=True, stop=True)
 
         def h_view(n):
-            return live["h", n][:].rearrange("p (t f) -> p f t", t=4)
+            return live["h", n][:].rearrange("p (e f) -> p f e", e=2)
 
         def count_turns(n):
-            turns = work.tile([P, P, 4], I32, name="turns", bufs=3)
+            turns = work.tile([P, 256, 2], I32, name="turns", bufs=3)
             live["turns", n] = turns
             nc.vector.tensor_scalar(out=turns[:], in0=h_view(n), scalar1=1.0 / (2.0 * math.pi), scalar2=0.25,
                                     op0=ALU.mult, op1=ALU.add)
 
         def reduce_angle(n):
             if n % 2 == 0:
-                live["angle", n // 2] = work.tile([P, 2, P, 4], F32, name="angle", bufs=2)
-            angle = live["angle", n // 2]
-            nc.vector.scalar_tensor_tensor(out=angle[:, n % 2], in0=live["turns", n][:], scalar=-2.0 * math.pi, in1=h_view(n),
-                                           op0=ALU.mult, op1=ALU.add)
+                live["angle", n // 2] = work.tile([P, 2, 256, 2], F32, name="angle", bufs=2)
+            nc.vector.scalar_tensor_tensor(out=live["angle", n // 2][:, n % 2], in0=live["turns", n][:], scalar=-2.0 * math.pi,
+                                           in1=h_view(n), op0=ALU.mult, op1=ALU.add)
 
-        def cosine(ft):
-            live["cos", ft] = work.tile([P, 2, P, 4], F32, name="cos", bufs=2)
-            nc.scalar.activation(out=live["cos", ft][:].rearrange("p g f t -> p (g f t)"),
-                                 in_=live["angle", ft][:].rearrange("p g f t -> p (g f t)"), func=ACT.Sin, bias=math.pi / 2.0)
+        def cosine(m):
+            live["cos", m] = work.tile([P, 1024], F32, name="cos", bufs=3)
+            nc.scalar.activation(out=live["cos", m][:].rearrange("p (f h e) -> p f h e", h=2, e=2),
+                                 in_=live["angle", m][:].rearrange("p h f e -> p f h e"), func=ACT.Sin, bias=math.pi / 2.0)
 
-        def apply_gain(ft):
-            z = work.tile([P, 2, P, 4], BF16, name="z", tag="z", bufs=1, align_bytes=64)
-            live["z", ft] = z
-            gains = gain_sb[:, ft : ft + 1, :] if ft < 2 else gain_sb[:]
-            engine = nc.gpsimd if D_ENG[ft] == "g" else nc.vector
-            engine.tensor_tensor(out=z[:], in0=live["cos", ft][:], in1=gains.unsqueeze(2).to_broadcast([P, 2, P, 4]),
-                                 op=ALU.mult)
+        def apply_gain(m, engine, lo, hi):
+            if engine == "g":
+                z = work.tile([P, 512 * (hi - lo)], BF16, name="z", bufs=1, align_bytes=64)
+            else:
+                z = work.tile([P, 512 * (hi - lo)], BF16, name="z_vector", bufs=2, align_bytes=64)
+            live["z", m, lo] = z
+            cols = slice(512 * lo, 512 * hi)
+            (nc.gpsimd if engine == "g" else nc.vector).tensor_tensor(out=z[:], in0=live["cos", m][:, cols], in1=gain_all[:, m % 2, cols], op=ALU.mult)
 
-        def quantize_z(ft):
-            quantize(z_codes[:, 256 * ft : 256 * (ft + 1)], z_scales[:, 256 * ft : 256 * (ft + 1)], live["z", ft][:].rearrange("p g f t -> p (g f t)"))
+        def quantize_z(m, lo, hi):
+            cols = slice(256 * m + P * lo, 256 * m + P * hi)
+            quantize(z_codes[:, cols], z_scales[:, cols], live["z", m, lo][:])
 
         def coupling(m):
-            q, h = ((0, 0), (1, 0), (2, 0), (0, 1), (3, 0), (1, 1), (2, 1), (3, 1))[m % 8]
+            q, h = ((0, 0), (1, 0), (0, 1), (1, 1), (2, 0), (3, 0), (2, 1), (3, 1))[m % 8]
             return 4 * (m // 8) + q, h
-
-        def lifting(n):
-            return (n % 2, n // 2) if n < 4 else divmod(n, 2)
-
-        def z_block(ft, g):
-            return 2 * g + ft if ft < 2 else 2 * ft + g
 
         def couple(m):
             ft, h = coupling(m)
             ps = bank("kt")
             live["kt", m] = ps
             for g in range(2):
-                zc = slice(P * z_block(ft, g), P * (z_block(ft, g) + 1))
+                block = 4 * (ft // 2) + 2 * g + ft % 2
+                zc = slice(P * block, P * (block + 1))
                 ac = slice(512 * h, 512 * (h + 1))
                 nc.tensor.matmul_mx(
                     out=ps[:], lhsT=z_codes[:, zc].bitcast(FP8X4), lhsT_scale=z_scales[:, zc],
@@ -225,7 +221,7 @@ def tile_network_koopman_step_h3_kernel(tc, x, w, gain, a, c, u, b, out_0, out_1
             ft, h = coupling(m)
             j, q = 2 * (ft // 4) + h, ft % 4
             if q == 0:
-                live["kc", j] = work.tile([P, 4, 512], F32, name="kc", bufs=4)
+                live["kc", j] = work.tile([P, 4, 512], F32, name="kc", bufs=3)
             if KC_ENG[m] == "s":
                 nc.scalar.activation(out=live["kc", j][:, q, :], in_=live["kt", m][:], func=ACT.Copy, scale=cu[:, ft : ft + 1])
             else:
@@ -249,17 +245,12 @@ def tile_network_koopman_step_h3_kernel(tc, x, w, gain, a, c, u, b, out_0, out_1
                 r0 = 512 * h + 128 * (s - 1)
                 nc.sync.dma_start(out=out_0[r0 : r0 + 256, 512 * G : 512 * (G + 1)].rearrange("(s p) f -> p s f", p=P), in_=y[:])
 
-        def round_y(engine, j, pair):
-            yb = work.tile([P, 1024], BF16, name="y_bf16", bufs=3)
-            live["yb", j, pair] = yb
-            dst = yb[:].rearrange("p (u q e) -> p u q e", u=2, e=2)
+        def round_y(engine, j, pair, lo, hi):
+            if ("yb", j, pair) not in live:
+                live["yb", j, pair] = work.tile([P, 1024], BF16, name="y_bf16", bufs=3)
+            dst = live["yb", j, pair][:].rearrange("p (u q e) -> p u q e", u=2, e=2)
             src = live["y", j, pair][:].rearrange("p s (q u e) -> p u (s q) e", u=2, e=2)
-            if engine == "gpsimd":
-                gpsimd_copy(dst, src)
-            elif engine == "scalar":
-                nc.scalar.copy(out=dst, in_=src)
-            else:
-                nc.vector.tensor_copy(out=dst, in_=src)
+            copies[engine](out=dst[:, :, lo:hi, :], in_=src[:, :, lo:hi, :])
 
         def turn_y(j, pair, tag):
             ps = bank(tag)
@@ -283,6 +274,8 @@ def tile_network_koopman_step_h3_kernel(tc, x, w, gain, a, c, u, b, out_0, out_1
                 live["last_ps", s] = ps
                 for uu in range(2):
                     nc.tensor.transpose(ps[:, P * uu : P * (uu + 1)], live["last", s][:].bitcast(F32)[:, P * uu : P * (uu + 1)], ident[:])
+
+        def finish_unload():
             for s in (2, 3):
                 dst = live["yg", 7][:].bitcast(F32)[:, 256 * s : 256 * (s + 1)].rearrange("p (m u) -> p m u", u=2)
                 copies["s" if s == 2 else "v"](out=dst, in_=live["last_ps", s][:, 0:256].rearrange("p (u m) -> p m u", u=2))
@@ -326,19 +319,39 @@ def tile_network_koopman_step_h3_kernel(tc, x, w, gain, a, c, u, b, out_0, out_1
             n = slot - lag
             return [n] if 0 <= n < count else []
 
+        interleave_w("v", 0, 0, 256)
+        quantize_x(0)
+        quantize_w(0, 0, 256)
         lift(0)
+        quantize_x(1)
         lift(1)
         for n in range(X_FIRST, 4):
             turn_x(n)
-        warm_up(int(WARM[0]))
+        spread_gain(1)
         interleave_w("v", 0, 256, 512)
         count_turns(0)
+        quantize_x(2)
+        lift(2)
         count_turns(1)
         reduce_angle(0)
-        quantize(x_codes[:, 1, :], x_scales[:, 1, :], x_grouped[1][:])
-        lift(2)
+        quantize_x(3)
         for slot in range(2, LAST_SLOT):
-            casts = [({"g": "gpsimd", "s": "scalar", "v": "vector"}[CASTS[n // 2]], n // 4, (n % 4) // 2) for n in due(slot, SUM_LAG + 1, 31) if n % 2 == 1]
+            casts = []
+            for n in due(slot, SUM_LAG + 1, 31):
+                if n % 2 == 1:
+                    how = CASTS[n // 2]
+                    if how in "gsv":
+                        casts.append((how, n // 4, (n % 4) // 2, 0, 256))
+                    else:
+                        casts.append(("g", n // 4, (n % 4) // 2, 0, 128))
+                        casts.append(("s" if how == "h" else "v", n // 4, (n % 4) // 2, 128, 256))
+            if slot % 2 == 0:
+                for n in due(slot, 6, 32):
+                    if D_ENG[n // 2] == "h":
+                        apply_gain(n // 2, "v", 1, 2)
+                for n in due(slot, 4, 32):
+                    if D_ENG[n // 2] == "v":
+                        apply_gain(n // 2, "v", 0, 2)
             for j in range(7):
                 if slot == SUM_LAG + 4 * j + QY_LAG[j]:
                     quantize_y(j, 0, 512)
@@ -357,16 +370,21 @@ def tile_network_koopman_step_h3_kernel(tc, x, w, gain, a, c, u, b, out_0, out_1
                 small_vectors()
             if slot % 2 == 0:
                 for n in due(slot, 6, 32):
-                    quantize_z(n // 2)
+                    if D_ENG[n // 2] == "h":
+                        quantize_z(n // 2, 1, 2)
+                        quantize_z(n // 2, 0, 1)
+                    else:
+                        quantize_z(n // 2, 0, 2)
             if slot % 2 == 0:
                 for n in due(slot, 4, 32):
-                    apply_gain(n // 2)
+                    if D_ENG[n // 2] != "v":
+                        apply_gain(n // 2, "g", 0, 1 if D_ENG[n // 2] == "h" else 2)
             for when, engine, G, lo, hi, when_q in W_PLAN:
                 if slot == when and engine == "g":
                     interleave_w(engine, G, lo, hi)
-            for engine, j, pair in casts:
-                if engine == "gpsimd":
-                    round_y(engine, j, pair)
+            for engine, j, pair, lo, hi in casts:
+                if engine == "g":
+                    round_y(engine, j, pair, lo, hi)
             for n in range(8):
                 if slot == A_SLOTS[n]:
                     turn_a(n)
@@ -380,8 +398,6 @@ def tile_network_koopman_step_h3_kernel(tc, x, w, gain, a, c, u, b, out_0, out_1
                     lift(n)
             for n in due(slot, KC_LAG - 1, 32):
                 couple(n)
-            if WARM[slot] != "0":
-                warm_up(int(WARM[slot]))
             if slot == 2:
                 reduce_angle(1)
                 quantize_w(0, 256, 512)
@@ -395,9 +411,9 @@ def tile_network_koopman_step_h3_kernel(tc, x, w, gain, a, c, u, b, out_0, out_1
             for n in due(slot, 2, 32):
                 if n % 2 == 1:
                     cosine(n // 2)
-            for engine, j, pair in casts:
-                if engine != "gpsimd":
-                    round_y(engine, j, pair)
+            for engine, j, pair, lo, hi in casts:
+                if engine != "g":
+                    round_y(engine, j, pair, lo, hi)
             for n in due(slot, KC_LAG, 32):
                 scale_c(n)
             for n in due(slot, SUM_LAG + 1 + TURN_LAG + UNLOAD_LAG, 31):
@@ -405,6 +421,8 @@ def tile_network_koopman_step_h3_kernel(tc, x, w, gain, a, c, u, b, out_0, out_1
                     unload_y(n // 4, (n % 4) // 2)
             if slot == SUM_LAG + 28 + LAST_LAG:
                 finish_last()
+            if slot == SUM_LAG + 28 + LAST_LAG + LAST_GAP:
+                finish_unload()
             for n in range(8):
                 if slot == A_SLOTS[n] + 1:
                     unload_a(n)

@@ -17,27 +17,37 @@ ALU = mybir.AluOpType
 ACT = mybir.ActivationFunctionType
 
 P = 128
-GAIN_ON_GPSIMD = True
-KC_LAG = 9
+GROUP = 512
+HALF = 256
+BANKS = 32
+UNITS = 16
+PANELS = 8
+PSUM_BUFS = {"lifted": 3, "coupled": 2, "turned": 2, "words": 1}
+
+GAIN_LAG = 4
+Z_LAG = 6
+SCALE_LAG = 9
 SUM_LAG = 16
-LAST_SLOT = 64
-X_FIRST = 3
-LAST_LAG = 4
-LAST_GAP = 2
-TAIL = 33
-A_SLOTS = (2, 3, 4, 4, 5, 7, 7, 8)
-A_Q = (5, 8, 10, 10)
-W_PLAN = ((3, 's', 1, 0, 256, 5), (6, 's', 1, 256, 512, 10), (9, 's', 2, 0, 256, 12), (11, 's', 2, 256, 512, 14), (14, 's', 3, 0, 256, 16), (15, 's', 3, 256, 512, 24))
-UNLOAD_ENG = 'ssssssvssssssssv'
-A_ENG = 'ssssssss'
-KC_ENG = 'ssssssssssssssssssssssssssssssss'
-VEC_SLOT = 6
-CASTS = 'hhsshsssvghhhgss'
-D_ENG = 'gggggggggggggggv'
-TURN_LAG = 2
-UNLOAD_LAG = 0
-QY_LAG = (12, 12, 10, 10, 9, 11, 8, 6, 9)
-LOADS = 'gxxwxwxawacwbw'
+ROUND_LAG = SUM_LAG + 1
+TURN_LAG = ROUND_LAG + 2
+Y_LAG = (12, 12, 12, 10, 8, 10, 11)
+LAST_FIRST_PAIR, LAST_ROUND, LAST_UNLOAD, LAST_SECOND_PAIR = 54, 50, 53, 55
+SLOTS = LAST_SECOND_PAIR + 1
+FREE_LIFT_BANKS = 33
+FREE_COUPLE_BANKS = SCALE_LAG + BANKS + 1
+EARLY_TURNS = (19, 20, 21, 22, 23, 26, 27, 28, 29, 30, 31)
+
+COUPLE_ORDER = ((0, 0), (1, 0), (0, 1), (1, 1), (2, 0), (3, 0), (2, 1), (3, 1))
+
+A_TURN_SLOTS = (2, 2, 3, 5, 6, 6, 7, 7)
+A_QUANTIZE_SLOTS = (6, 8, 10, 10)
+W_SLOTS = ((3, 6), (5, 8), (10, 14), (11, 16), (15, 20), (19, 22))
+W_SECOND_HALF_SLOT = 3
+VECTORS_SLOT = 8
+
+ROUND_ENGINE = "sssssssssshghgs"
+SCALE_ON_VECTOR = (23, 24, 28)
+UNLOAD_ON_VECTOR = 14
 
 
 def tile_network_koopman_step_h3_kernel(tc, x, w, gain, a, c, u, b, out_0, out_1, out_2):
@@ -47,385 +57,399 @@ def tile_network_koopman_step_h3_kernel(tc, x, w, gain, a, c, u, b, out_0, out_1
         work = ctx.enter_context(tc.tile_pool(name="work", bufs=2))
         psum = ctx.enter_context(tc.psum_pool(name="psum", bufs=2))
         ctx.enter_context(tc.manual_schedule())
+        live = {}
 
         def bank(tag):
-            return psum.tile([P, 512], F32, name=tag, tag=tag, bufs={"h": 3, "kt": 2, "tn": 2, "wt": 1}[tag])
+            return psum.tile([P, GROUP], F32, name=tag, tag=tag, bufs=PSUM_BUFS[tag])
 
-        def quantize(codes, scales, src):
-            nc.vector.quantize_mx(out=codes.bitcast(FP8X4), scales=scales, in_=src)
+        def quantize(codes, scales, grouped):
+            nc.vector.quantize_mx(out=codes.bitcast(FP8X4), scales=scales, in_=grouped)
 
-        x_raw = [keep.tile([P, 2, D], BF16, name="x_raw%d" % n) for n in range(4)]
-        w_raw = [keep.tile([P, 4, 512], BF16, name="w_raw%d" % G) for G in range(4)]
+        def gpsimd_copy(out, in_):
+            nc.gpsimd.tensor_scalar(out=out, in0=in_, scalar1=1.0, scalar2=1.0, op0=ALU.mult, op1=ALU.mult)
+
+        copies = {"g": gpsimd_copy, "s": nc.scalar.copy, "v": nc.vector.tensor_copy}
+
+        x_raw = [keep.tile([P, 2, D], BF16, name="x_raw%d" % piece) for piece in range(4)]
+        w_raw = [keep.tile([P, 4, GROUP], BF16, name="w_raw%d" % og) for og in range(4)]
         a_raw = [keep.tile([P, 4, S], BF16, name="a_raw%d" % h) for h in range(2)]
-        gain_sb = keep.tile([P, 2, 4], BF16)
+        gain_raw = keep.tile([P, 2, 4], BF16)
         rows = keep.tile([P, P], BF16)
         b_all = keep.tile([P, F], BF16)
         ident = keep.tile([P, P], F32)
         warm = keep.tile([P, 1], F32)
 
-        def load_x(n):
-            g, pair = divmod(n, 2)
-            rows_g = x[512 * g : 512 * (g + 1), :].rearrange("(p t) d -> p t d", t=4)
-            nc.sync.dma_start(out=x_raw[n][:], in_=rows_g[:, 2 * pair : 2 * pair + 2, :])
+        def load_x(piece):
+            g, pair = divmod(piece, 2)
+            sites = x[GROUP * g : GROUP * (g + 1), :].rearrange("(p t) d -> p t d", t=4)
+            nc.sync.dma_start(out=x_raw[piece][:], in_=sites[:, 2 * pair : 2 * pair + 2, :])
 
-        def load_w(G, lo=0, hi=512):
-            nc.sync.dma_start(out=w_raw[G][:, :, lo:hi], in_=w[:, 512 * G + lo : 512 * G + hi].rearrange("(p j) f -> p j f", j=4))
+        def load_w(og, lo, hi):
+            cols = slice(GROUP * og + lo, GROUP * og + hi)
+            nc.sync.dma_start(out=w_raw[og][:, :, lo:hi], in_=w[:, cols].rearrange("(p t) f -> p t f", t=4))
 
         def load_a(h):
-            nc.sync.dma_start(out=a_raw[h][:], in_=a[512 * h : 512 * (h + 1), :].rearrange("(s p) k -> p s k", p=P))
+            nc.sync.dma_start(out=a_raw[h][:], in_=a[GROUP * h : GROUP * (h + 1), :].rearrange("(s p) k -> p s k", p=P))
 
         nc.vector.memset(rows[:], 0.0)
         make_identity(nc, ident[:])
         nc.scalar.activation(out=warm[:], in_=rows[:, 0:1], func=ACT.Sin)
-        count = {"x": 0, "w": 0, "a": 0}
-        for kind in LOADS:
-            if kind == "x":
-                load_x(count["x"])
-            elif kind == "a":
-                load_a(count["a"])
-            elif kind == "w":
-                load_w(*((0, 0, 256), (0, 256, 512), (1,), (2,), (3,))[count["w"]])
-            elif kind == "g":
-                nc.sync.dma_start(out=gain_sb[:], in_=gain.rearrange("(g p t) -> p g t", g=2, t=4))
-            elif kind == "c":
-                nc.sync.dma_start(out=rows[0:16, :], in_=c.rearrange("(r p) -> r p", p=P))
-                nc.sync.dma_start(out=rows[16:24, :], in_=u.rearrange("(r p) -> r p", p=P))
-            else:
-                nc.sync.dma_start(out=b_all[:], in_=b.partition_broadcast(P))
-            if kind in count:
-                count[kind] += 1
+        load_x(0)
+        nc.sync.dma_start(out=gain_raw[:], in_=gain.rearrange("(g p t) -> p g t", g=2, t=4))
+        load_x(1)
+        load_w(0, 0, HALF)
+        load_x(2)
+        load_x(3)
+        load_w(0, HALF, GROUP)
+        load_a(0)
+        load_w(1, 0, GROUP)
+        load_w(2, 0, GROUP)
+        load_a(1)
+        nc.sync.dma_start(out=rows[0:16, :], in_=c.rearrange("(r p) -> r p", p=P))
+        nc.sync.dma_start(out=rows[16:24, :], in_=u.rearrange("(r p) -> r p", p=P))
+        load_w(3, 0, GROUP)
+        nc.sync.dma_start(out=b_all[:], in_=b.partition_broadcast(P))
 
-        gain_all = keep.tile([P, 2, 1024], F32)
+        gain_all = keep.tile([P, 2, 4 * HALF], F32)
+        for g in range(2):
+            nc.vector.tensor_copy(
+                out=gain_all[:, g, :].rearrange("p (f t) -> p f t", t=4),
+                in_=gain_raw[:, g : g + 1, :].to_broadcast([P, HALF, 4]),
+            )
 
-        def spread_gain(g):
-            nc.scalar.copy(out=gain_all[:, g, :].rearrange("p (f t) -> p f t", t=4), in_=gain_sb[:, g : g + 1, :].to_broadcast([P, 256, 4]))
-
-        spread_gain(0)
-        x_codes = keep.tile([P, 2, 512], U32, align_bytes=64)
-        x_scales = keep.tile([P, 2, 512], U8, align_bytes=64)
+        x_codes = keep.tile([P, 2, GROUP], U32, align_bytes=64)
+        x_scales = keep.tile([P, 2, GROUP], U8, align_bytes=64)
         w_codes = keep.tile([P, F], U32, align_bytes=64)
         w_scales = keep.tile([P, F], U8, align_bytes=64)
         a_codes = keep.tile([P, 2, S], U32, align_bytes=64)
         a_scales = keep.tile([P, 2, S], U8, align_bytes=64)
-        z_codes = keep.tile([P, 32 * P], U32, align_bytes=64)
-        z_scales = keep.tile([P, 32 * P], U8, align_bytes=64)
+        z_codes = keep.tile([P, UNITS * HALF], U32, align_bytes=64)
+        z_scales = keep.tile([P, UNITS * HALF], U8, align_bytes=64)
         y_scales = keep.tile([P, 4, S], U8, align_bytes=64)
-        rows32 = keep.tile([P, P], F32)
+        rows_f32 = keep.tile([P, P], F32)
         cu = keep.tile([P, 32], F32)
-        live = {}
+        x_grouped = [keep.tile([P, 4 * GROUP], BF16, name="x_grouped%d" % g, align_bytes=64) for g in range(2)]
 
-        def turn_words(ps, sources):
-            view = ps[:].rearrange("p (s u m) -> p s u m", s=2, u=2)
-            for s2 in range(2):
-                for uu in range(2):
-                    nc.tensor.transpose(view[:, s2, uu, :], sources(s2, uu), ident[:])
+        def turn_words(ps, source):
+            view = ps[:].rearrange("p (s e m) -> p s e m", s=2, e=2)
+            for s in range(2):
+                for e in range(2):
+                    nc.tensor.transpose(view[:, s, e, :], source(s, e), ident[:])
 
-        def unload_words(engine_copy, grouped, pair, ps):
-            dst = grouped[:].bitcast(F32)[:, 512 * pair : 512 * (pair + 1)].rearrange("p (s m u) -> p s m u", s=2, u=2)
-            engine_copy(out=dst, in_=ps[:].rearrange("p (s u m) -> p s m u", s=2, u=2))
+        def unload_words(engine, grouped, pair, ps):
+            words = grouped[:].bitcast(F32)[:, GROUP * pair : GROUP * (pair + 1)]
+            copies[engine](
+                out=words.rearrange("p (s m e) -> p s m e", s=2, e=2), in_=ps[:].rearrange("p (s e m) -> p s m e", s=2, e=2)
+            )
 
-        def gpsimd_copy(out, in_):
-            nc.gpsimd.tensor_scalar(out=out, in0=in_, scalar1=1.0, scalar2=1.0, op0=ALU.mult, op1=ALU.mult)
+        def turn_x(piece):
+            ps = bank("turned" if piece < 2 else "coupled")
+            words = x_raw[piece][:].bitcast(F32)
+            turn_words(ps, lambda s, e: words[:, s, e:256:2])
+            unload_words("s", x_grouped[piece // 2], piece % 2, ps)
 
-        def interleave_w(engine, G, lo, hi):
-            if engine == "g":
-                grouped = work.tile([P, 4 * (hi - lo)], BF16, name="w_grouped_g", bufs=2, align_bytes=64)
-            else:
-                grouped = work.tile([P, 4 * (hi - lo)], BF16, name="w_grouped", bufs=2, align_bytes=64)
-            live["wg", G, lo] = grouped
-            copies[engine](out=grouped[:].rearrange("p (f j) -> p f j", j=4), in_=w_raw[G][:, :, lo:hi].rearrange("p j f -> p f j"))
-
-        def quantize_w(G, lo, hi):
-            cols = slice(512 * G + lo, 512 * G + hi)
-            quantize(w_codes[:, cols], w_scales[:, cols], live["wg", G, lo][:])
-
-        copies = {"g": gpsimd_copy, "s": nc.scalar.copy, "v": nc.vector.tensor_copy}
-
-        x_grouped = [keep.tile([P, 2048], BF16, name="x_grouped0", align_bytes=64),
-                     keep.tile([P, 2048], BF16, name="x_grouped1", align_bytes=64)]
-
-        def turn_x(n):
-            ps = bank("tn" if n < 2 else "kt")
-            words = x_raw[n][:].bitcast(F32)
-            turn_words(ps, lambda s2, uu: words[:, s2, uu:256:2])
-            unload_words(nc.scalar.copy, x_grouped[n // 2], n % 2, ps)
-
-        for n in range(X_FIRST):
-            turn_x(n)
-
-        def quantize_x(n):
-            g, cols = n // 2, slice(256 * (n % 2), 256 * (n % 2 + 1))
-            quantize(x_codes[:, g, cols], x_scales[:, g, cols], x_grouped[g][:, 1024 * (n % 2) : 1024 * (n % 2 + 1)])
-
-        def lift(n):
-            fh, g, pair = n // 4, (n // 2) % 2, n % 2
-            ps = bank("h")
-            live["h", n] = ps
-            wc = slice(256 * fh, 256 * (fh + 1))
-            for e in range(2):
-                xc = slice(P * (2 * pair + e), P * (2 * pair + e + 1))
-                nc.tensor.matmul_mx(
-                    out=ps[:, 256 * e : 256 * (e + 1)], lhsT=x_codes[:, g, xc].bitcast(FP8X4), lhsT_scale=x_scales[:, g, xc],
-                    rhs=w_codes[:, wc].bitcast(FP8X4), rhs_scale=w_scales[:, wc], start=True, stop=True)
-
-        def h_view(n):
-            return live["h", n][:].rearrange("p (e f) -> p f e", e=2)
-
-        def count_turns(n):
-            turns = work.tile([P, 256, 2], I32, name="turns", bufs=3)
-            live["turns", n] = turns
-            nc.vector.tensor_scalar(out=turns[:], in0=h_view(n), scalar1=1.0 / (2.0 * math.pi), scalar2=0.25,
-                                    op0=ALU.mult, op1=ALU.add)
-
-        def reduce_angle(n):
-            if n % 2 == 0:
-                live["angle", n // 2] = work.tile([P, 2, 256, 2], F32, name="angle", bufs=2)
-            nc.vector.scalar_tensor_tensor(out=live["angle", n // 2][:, n % 2], in0=live["turns", n][:], scalar=-2.0 * math.pi,
-                                           in1=h_view(n), op0=ALU.mult, op1=ALU.add)
-
-        def cosine(m):
-            live["cos", m] = work.tile([P, 1024], F32, name="cos", bufs=3)
-            nc.scalar.activation(out=live["cos", m][:].rearrange("p (f h e) -> p f h e", h=2, e=2),
-                                 in_=live["angle", m][:].rearrange("p h f e -> p f h e"), func=ACT.Sin, bias=math.pi / 2.0)
-
-        def apply_gain(m, engine, lo, hi):
-            if engine == "g":
-                z = work.tile([P, 512 * (hi - lo)], BF16, name="z", bufs=1, align_bytes=64)
-            else:
-                z = work.tile([P, 512 * (hi - lo)], BF16, name="z_vector", bufs=2, align_bytes=64)
-            live["z", m, lo] = z
-            cols = slice(512 * lo, 512 * hi)
-            (nc.gpsimd if engine == "g" else nc.vector).tensor_tensor(out=z[:], in0=live["cos", m][:, cols], in1=gain_all[:, m % 2, cols], op=ALU.mult)
-
-        def quantize_z(m, lo, hi):
-            cols = slice(256 * m + P * lo, 256 * m + P * hi)
-            quantize(z_codes[:, cols], z_scales[:, cols], live["z", m, lo][:])
-
-        def coupling(m):
-            q, h = ((0, 0), (1, 0), (0, 1), (1, 1), (2, 0), (3, 0), (2, 1), (3, 1))[m % 8]
-            return 4 * (m // 8) + q, h
-
-        def couple(m):
-            ft, h = coupling(m)
-            ps = bank("kt")
-            live["kt", m] = ps
-            for g in range(2):
-                block = 4 * (ft // 2) + 2 * g + ft % 2
-                zc = slice(P * block, P * (block + 1))
-                ac = slice(512 * h, 512 * (h + 1))
-                nc.tensor.matmul_mx(
-                    out=ps[:], lhsT=z_codes[:, zc].bitcast(FP8X4), lhsT_scale=z_scales[:, zc],
-                    rhs=a_codes[:, g, ac].bitcast(FP8X4), rhs_scale=a_scales[:, g, ac], start=(g == 0), stop=(g == 1))
-
-        def scale_c(m):
-            ft, h = coupling(m)
-            j, q = 2 * (ft // 4) + h, ft % 4
-            if q == 0:
-                live["kc", j] = work.tile([P, 4, 512], F32, name="kc", bufs=3)
-            if KC_ENG[m] == "s":
-                nc.scalar.activation(out=live["kc", j][:, q, :], in_=live["kt", m][:], func=ACT.Copy, scale=cu[:, ft : ft + 1])
-            else:
-                nc.vector.tensor_scalar(out=live["kc", j][:, q, :], in0=live["kt", m][:], scalar1=cu[:, ft : ft + 1], scalar2=None, op0=ALU.mult)
-
-        def turn_kc(j, s, tag):
-            ps = bank(tag)
-            live["tn", j, s] = ps
-            for q in range(4):
-                nc.tensor.transpose(ps[:, 128 * q : 128 * (q + 1)], live["kc", j][:, q, 128 * s : 128 * (s + 1)], ident[:])
-
-        def add_control(j, s):
-            G, h = divmod(j, 2)
-            if s % 2 == 0:
-                live["y", j, s // 2] = work.tile([P, 2, 512], F32, name="y", bufs=4)
-            y = live["y", j, s // 2]
-            col = 16 + 4 * h + s
-            nc.vector.scalar_tensor_tensor(out=y[:, s % 2, :], in0=b_all[:, 512 * G : 512 * (G + 1)], scalar=cu[:, col : col + 1],
-                                           in1=live["tn", j, s][:], op0=ALU.mult, op1=ALU.add)
-            if s % 2 == 1:
-                r0 = 512 * h + 128 * (s - 1)
-                nc.sync.dma_start(out=out_0[r0 : r0 + 256, 512 * G : 512 * (G + 1)].rearrange("(s p) f -> p s f", p=P), in_=y[:])
-
-        def round_y(engine, j, pair, lo, hi):
-            if ("yb", j, pair) not in live:
-                live["yb", j, pair] = work.tile([P, 1024], BF16, name="y_bf16", bufs=3)
-            dst = live["yb", j, pair][:].rearrange("p (u q e) -> p u q e", u=2, e=2)
-            src = live["y", j, pair][:].rearrange("p s (q u e) -> p u (s q) e", u=2, e=2)
-            copies[engine](out=dst[:, :, lo:hi, :], in_=src[:, :, lo:hi, :])
-
-        def turn_y(j, pair, tag):
-            ps = bank(tag)
-            live["wt", j, pair] = ps
-            words = live["yb", j, pair][:].bitcast(F32)
-            turn_words(ps, lambda s2, uu: words[:, 256 * uu + 128 * s2 : 256 * uu + 128 * (s2 + 1)])
-
-        def unload_y(j, pair):
-            if pair == 0:
-                live["yg", j] = work.tile([P, 2048], BF16, name="y_grouped", align_bytes=64)
-            unload_words(copies[UNLOAD_ENG[2 * j + pair]], live["yg", j], pair, live["wt", j, pair])
-
-        def finish_last():
-            for s in (2, 3):
-                yb = work.tile([P, 512], BF16, name="y_bf16_last")
-                live["last", s] = yb
-                copies["s" if s == 2 else "v"](out=yb[:].rearrange("p (u q e) -> p u q e", u=2, e=2),
-                                               in_=live["y", 7, 1][:, s % 2, :].rearrange("p (q u e) -> p u q e", u=2, e=2))
-            for s in (2, 3):
-                ps = bank("kt")
-                live["last_ps", s] = ps
-                for uu in range(2):
-                    nc.tensor.transpose(ps[:, P * uu : P * (uu + 1)], live["last", s][:].bitcast(F32)[:, P * uu : P * (uu + 1)], ident[:])
-
-        def finish_unload():
-            for s in (2, 3):
-                dst = live["yg", 7][:].bitcast(F32)[:, 256 * s : 256 * (s + 1)].rearrange("p (m u) -> p m u", u=2)
-                copies["s" if s == 2 else "v"](out=dst, in_=live["last_ps", s][:, 0:256].rearrange("p (u m) -> p m u", u=2))
-
-        def quantize_y(j, lo, hi):
-            G, h = divmod(j, 2)
-            codes = work.tile([P, hi - lo], U32, name="y_codes", bufs=3, align_bytes=64)
-            cols = slice(512 * h + lo, 512 * h + hi)
-            quantize(codes[:], y_scales[:, G, cols], live["yg", j][:, 4 * lo : 4 * hi])
-            nc.sync.dma_start(out=out_1[G, :, cols, :].rearrange("p m t -> p (m t)").bitcast(I32), in_=codes[:].bitcast(I32))
-            if h == 1 and hi == 512:
-                for Q in range(4):
-                    queue = nc.scalar if j == 7 and Q % 2 == 1 else nc.sync
-                    queue.dma_start(out=out_2[G, 4 * Q : 4 * Q + 4, :].bitcast(I32),
-                                    in_=y_scales[32 * Q : 32 * Q + 4, G, :].bitcast(I32))
+        def quantize_x(piece):
+            g, pair = divmod(piece, 2)
+            cols = slice(HALF * pair, HALF * (pair + 1))
+            quantize(x_codes[:, g, cols], x_scales[:, g, cols], x_grouped[g][:, 4 * HALF * pair : 4 * HALF * (pair + 1)])
 
         def turn_a(n):
             h, g, pair = n // 4, (n // 2) % 2, n % 2
-            ps = bank("kt" if n > 0 and A_SLOTS[n] == A_SLOTS[n - 1] else "tn")
-            live["at", n] = ps
+            second_of_slot = n > 0 and A_TURN_SLOTS[n] == A_TURN_SLOTS[n - 1]
+            live["a_words", n] = bank("coupled" if second_of_slot else "turned")
             words = a_raw[h][:].bitcast(F32)
-            turn_words(ps, lambda s2, uu: words[:, 2 * pair + s2, 256 * g + uu : 256 * (g + 1) : 2])
+            turn_words(live["a_words", n], lambda s, e: words[:, 2 * pair + s, 256 * g + e : 256 * (g + 1) : 2])
 
         def unload_a(n):
             if n % 2 == 0:
-                live["ag", n // 2] = work.tile([P, 2048], BF16, name="a_grouped", align_bytes=64)
-            unload_words(copies[A_ENG[n]], live["ag", n // 2], n % 2, live["at", n])
+                live["a_grouped", n // 2] = work.tile([P, 4 * GROUP], BF16, name="a_grouped", align_bytes=64)
+            unload_words("s", live["a_grouped", n // 2], n % 2, live["a_words", n])
 
-        def quantize_a(m):
-            h, g = divmod(m, 2)
-            cols = slice(512 * h, 512 * (h + 1))
-            quantize(a_codes[:, g, cols], a_scales[:, g, cols], live["ag", m][:])
+        def quantize_a(part):
+            h, g = divmod(part, 2)
+            cols = slice(GROUP * h, GROUP * (h + 1))
+            quantize(a_codes[:, g, cols], a_scales[:, g, cols], live["a_grouped", part][:])
 
-        def small_vectors():
-            nc.scalar.copy(out=rows32[:], in_=rows[:])
-            ps = bank("wt")
-            nc.tensor.transpose(ps[:, 0:P], rows32[:], ident[:])
+        def interleave_w(engine, half):
+            og, lo = half // 2, HALF * (half % 2)
+            live["w_grouped", half] = work.tile([P, 4 * HALF], BF16, name="w_grouped", align_bytes=64)
+            copies[engine](
+                out=live["w_grouped", half][:].rearrange("p (f i t) -> p f t i", i=4, t=4),
+                in_=w_raw[og][:, :, lo : lo + HALF].rearrange("p t (f i) -> p f t i", i=4),
+            )
+
+        def quantize_w(half):
+            cols = slice(HALF * half, HALF * (half + 1))
+            quantize(w_codes[:, cols], w_scales[:, cols], live["w_grouped", half][:])
+
+        def vectors_onto_partitions():
+            nc.scalar.copy(out=rows_f32[:], in_=rows[:])
+            ps = bank("words")
+            nc.tensor.transpose(ps[:, 0:P], rows_f32[:], ident[:])
             nc.scalar.copy(out=cu[:], in_=ps[:, 0:32])
 
-        def due(slot, lag, count):
-            n = slot - lag
-            return [n] if 0 <= n < count else []
+        def lift(n):
+            half, g, pair = n // 4, (n // 2) % 2, n % 2
+            live["h", n] = bank("lifted")
+            w_cols = slice(HALF * half, HALF * (half + 1))
+            for e in range(2):
+                x_cols = slice(P * (2 * pair + e), P * (2 * pair + e + 1))
+                nc.tensor.matmul_mx(
+                    out=live["h", n][:, HALF * e : HALF * (e + 1)],
+                    lhsT=x_codes[:, g, x_cols].bitcast(FP8X4),
+                    lhsT_scale=x_scales[:, g, x_cols],
+                    rhs=w_codes[:, w_cols].bitcast(FP8X4),
+                    rhs_scale=w_scales[:, w_cols],
+                    start=True,
+                    stop=True,
+                )
 
-        interleave_w("v", 0, 0, 256)
+        def h_pairs(n):
+            return live["h", n][:].rearrange("p (e f) -> p f e", e=2)
+
+        def count_turns(n):
+            live["turns", n] = work.tile([P, HALF, 2], I32, name="turns", bufs=3)
+            nc.vector.tensor_scalar(
+                out=live["turns", n][:], in0=h_pairs(n), scalar1=1.0 / (2.0 * math.pi), scalar2=0.25, op0=ALU.mult, op1=ALU.add
+            )
+
+        def reduce_angle(n):
+            if n % 2 == 0:
+                live["angle", n // 2] = work.tile([P, 2, HALF, 2], F32, name="angle")
+            nc.vector.scalar_tensor_tensor(
+                out=live["angle", n // 2][:, n % 2],
+                in0=live["turns", n][:],
+                scalar=-2.0 * math.pi,
+                in1=h_pairs(n),
+                op0=ALU.mult,
+                op1=ALU.add,
+            )
+
+        def cosine(m):
+            live["cos", m] = work.tile([P, 4 * HALF], F32, name="cos", bufs=3)
+            nc.scalar.activation(
+                out=live["cos", m][:].rearrange("p (f pair e) -> p f pair e", pair=2, e=2),
+                in_=live["angle", m][:].rearrange("p pair f e -> p f pair e"),
+                func=ACT.Sin,
+                bias=math.pi / 2.0,
+            )
+
+        def apply_gain(m):
+            last = m == UNITS - 1
+            live["z", m] = work.tile([P, 4 * HALF], BF16, name="z_last" if last else "z", bufs=1, align_bytes=64)
+            engine = nc.vector if last else nc.gpsimd
+            engine.tensor_tensor(out=live["z", m][:], in0=live["cos", m][:], in1=gain_all[:, m % 2, :], op=ALU.mult)
+
+        def quantize_z(m):
+            cols = slice(HALF * m, HALF * (m + 1))
+            quantize(z_codes[:, cols], z_scales[:, cols], live["z", m][:])
+
+        def couple(n):
+            q, h = COUPLE_ORDER[n % 8]
+            tile = 4 * (n // 8) + q
+            live["kt", n] = bank("coupled")
+            a_cols = slice(GROUP * h, GROUP * (h + 1))
+            for g in range(2):
+                first = HALF * (2 * (tile // 2) + g) + P * (tile % 2)
+                nc.tensor.matmul_mx(
+                    out=live["kt", n][:],
+                    lhsT=z_codes[:, first : first + P].bitcast(FP8X4),
+                    lhsT_scale=z_scales[:, first : first + P],
+                    rhs=a_codes[:, g, a_cols].bitcast(FP8X4),
+                    rhs_scale=a_scales[:, g, a_cols],
+                    start=(g == 0),
+                    stop=(g == 1),
+                )
+
+        def scale_by_c(n):
+            q, h = COUPLE_ORDER[n % 8]
+            j, tile = 2 * (n // 8) + h, 4 * (n // 8) + q
+            if q == 0:
+                live["kc", j] = work.tile([P, 4, GROUP], F32, name="kc", bufs=3)
+            dst, c_col = live["kc", j][:, q, :], cu[:, tile : tile + 1]
+            if n in SCALE_ON_VECTOR:
+                nc.vector.tensor_scalar(out=dst, in0=live["kt", n][:], scalar1=c_col, scalar2=None, op0=ALU.mult)
+            else:
+                nc.scalar.activation(out=dst, in_=live["kt", n][:], func=ACT.Copy, scale=c_col)
+
+        def turn_kc(n, tag):
+            j, s = divmod(n, 4)
+            live["kc_turned", n] = bank(tag)
+            for q in range(4):
+                nc.tensor.transpose(live["kc_turned", n][:, P * q : P * (q + 1)], live["kc", j][:, q, P * s : P * (s + 1)], ident[:])
+
+        def add_control(n):
+            og, site_tile = divmod(n, 8)
+            if n % 2 == 0:
+                live["y", n // 2] = work.tile([P, 2, GROUP], F32, name="y", bufs=4)
+            y = live["y", n // 2]
+            cols = slice(GROUP * og, GROUP * (og + 1))
+            nc.vector.scalar_tensor_tensor(
+                out=y[:, n % 2, :],
+                in0=b_all[:, cols],
+                scalar=cu[:, 16 + site_tile : 17 + site_tile],
+                in1=live["kc_turned", n][:],
+                op0=ALU.mult,
+                op1=ALU.add,
+            )
+            if n >= BANKS - 2:
+                nc.sync.dma_start(out=out_0[P * site_tile : P * (site_tile + 1), cols], in_=y[:, n % 2, :])
+            elif n % 2 == 1:
+                sites = slice(P * (site_tile - 1), P * (site_tile + 1))
+                nc.sync.dma_start(out=out_0[sites, cols].rearrange("(s p) f -> p s f", p=P), in_=y[:])
+
+        def round_y(engine, i, lo, hi):
+            if ("y_bf16", i) not in live:
+                live["y_bf16", i] = work.tile([P, 2 * GROUP], BF16, name="y_bf16", bufs=3)
+            dst = live["y_bf16", i][:].rearrange("p (e q v) -> p e q v", e=2, v=2)
+            src = live["y", i][:].rearrange("p s (q e v) -> p e (s q) v", e=2, v=2)
+            copies[engine](out=dst[:, :, lo:hi, :], in_=src[:, :, lo:hi, :])
+
+        def turn_y(i, tag):
+            live["y_words", i] = bank(tag)
+            words = live["y_bf16", i][:].bitcast(F32)
+            turn_words(live["y_words", i], lambda s, e: words[:, 256 * e + P * s : 256 * e + P * (s + 1)])
+
+        def unload_y(i):
+            if i % 2 == 0:
+                live["y_grouped", i // 2] = work.tile([P, 4 * GROUP], BF16, name="y_grouped", align_bytes=64)
+            unload_words("v" if i == UNLOAD_ON_VECTOR else "s", live["y_grouped", i // 2], i % 2, live["y_words", i])
+
+        def round_and_turn_last_pair():
+            for s in range(2):
+                live["last_bf16", s] = work.tile([P, GROUP], BF16, name="last_bf16")
+                copies["sv"[s]](
+                    out=live["last_bf16", s][:].rearrange("p (e q v) -> p e q v", e=2, v=2),
+                    in_=live["y", 2 * PANELS - 1][:, s, :].rearrange("p (q e v) -> p e q v", e=2, v=2),
+                )
+            for s in range(2):
+                live["last_words", s] = bank("coupled")
+                words = live["last_bf16", s][:].bitcast(F32)
+                for e in range(2):
+                    nc.tensor.transpose(live["last_words", s][:, P * e : P * (e + 1)], words[:, P * e : P * (e + 1)], ident[:])
+
+        def unload_last_pair():
+            for s in range(2):
+                words = live["y_grouped", PANELS - 1][:].bitcast(F32)[:, 256 * (2 + s) : 256 * (3 + s)]
+                copies["sv"[s]](
+                    out=words.rearrange("p (m e) -> p m e", e=2),
+                    in_=live["last_words", s][:, 0:256].rearrange("p (e m) -> p m e", e=2),
+                )
+
+        def quantize_y(j, lo, hi):
+            og, h = divmod(j, 2)
+            very_last = j == PANELS - 1 and hi == GROUP
+            codes = work.tile([P, hi - lo], U32, name="y_codes", bufs=4, align_bytes=64)
+            sites = slice(GROUP * h + lo, GROUP * h + hi)
+            quantize(codes[:], y_scales[:, og, sites], live["y_grouped", j][:, 4 * lo : 4 * hi])
+            queue = nc.scalar if very_last else nc.sync
+            queue.dma_start(out=out_1[og, :, sites, :].rearrange("p m t -> p (m t)").bitcast(I32), in_=codes[:].bitcast(I32))
+            if h == 1 and hi == GROUP:
+                for quad in range(4):
+                    queue = nc.scalar if very_last and quad % 2 == 1 else nc.sync
+                    queue.dma_start(
+                        out=out_2[og, 4 * quad : 4 * quad + 4, :].bitcast(I32),
+                        in_=y_scales[32 * quad : 32 * quad + 4, og, :].bitcast(I32),
+                    )
+
+        def behind(slot, lag, count):
+            return [slot - lag] if 0 <= slot - lag < count else []
+
+        def pair_behind(slot, lag, count):
+            return [n // 2 for n in behind(slot, lag, 2 * count) if n % 2 == 1]
+
+        for piece in range(3):
+            turn_x(piece)
+        interleave_w("v", 0)
         quantize_x(0)
-        quantize_w(0, 0, 256)
+        quantize_w(0)
         lift(0)
         quantize_x(1)
         lift(1)
-        for n in range(X_FIRST, 4):
-            turn_x(n)
-        spread_gain(1)
-        interleave_w("v", 0, 256, 512)
+        turn_x(3)
+        interleave_w("s", 1)
         count_turns(0)
         quantize_x(2)
         lift(2)
         count_turns(1)
         reduce_angle(0)
         quantize_x(3)
-        for slot in range(2, LAST_SLOT):
-            casts = []
-            for n in due(slot, SUM_LAG + 1, 31):
-                if n % 2 == 1:
-                    how = CASTS[n // 2]
-                    if how in "gsv":
-                        casts.append((how, n // 4, (n % 4) // 2, 0, 256))
-                    else:
-                        casts.append(("g", n // 4, (n % 4) // 2, 0, 128))
-                        casts.append(("s" if how == "h" else "v", n // 4, (n % 4) // 2, 128, 256))
-            if slot % 2 == 0:
-                for n in due(slot, 6, 32):
-                    if D_ENG[n // 2] == "h":
-                        apply_gain(n // 2, "v", 1, 2)
-                for n in due(slot, 4, 32):
-                    if D_ENG[n // 2] == "v":
-                        apply_gain(n // 2, "v", 0, 2)
-            for j in range(7):
-                if slot == SUM_LAG + 4 * j + QY_LAG[j]:
-                    quantize_y(j, 0, 512)
-            for pair in range(2):
-                if slot == SUM_LAG + 28 + QY_LAG[7 + pair]:
-                    quantize_y(7, 256 * pair, 256 * (pair + 1))
-            for when, engine, G, lo, hi, when_q in W_PLAN:
-                if slot == when and engine == "v":
-                    interleave_w(engine, G, lo, hi)
-                if slot == when_q:
-                    quantize_w(G, lo, hi)
-            for m in range(4):
-                if slot == A_Q[m]:
-                    quantize_a(m)
-            if slot == VEC_SLOT:
-                small_vectors()
-            if slot % 2 == 0:
-                for n in due(slot, 6, 32):
-                    if D_ENG[n // 2] == "h":
-                        quantize_z(n // 2, 1, 2)
-                        quantize_z(n // 2, 0, 1)
-                    else:
-                        quantize_z(n // 2, 0, 2)
-            if slot % 2 == 0:
-                for n in due(slot, 4, 32):
-                    if D_ENG[n // 2] != "v":
-                        apply_gain(n // 2, "g", 0, 1 if D_ENG[n // 2] == "h" else 2)
-            for when, engine, G, lo, hi, when_q in W_PLAN:
-                if slot == when and engine == "g":
-                    interleave_w(engine, G, lo, hi)
-            for engine, j, pair, lo, hi in casts:
+
+        for slot in range(2, SLOTS):
+            roundings = []
+            for i in pair_behind(slot, ROUND_LAG, 2 * PANELS - 1):
+                if ROUND_ENGINE[i] == "h":
+                    roundings.extend([("g", i, 0, P), ("s", i, P, 2 * P)])
+                else:
+                    roundings.append((ROUND_ENGINE[i], i, 0, 2 * P))
+
+            if slot == 2 * (UNITS - 1) + GAIN_LAG:
+                apply_gain(UNITS - 1)
+            for j in range(PANELS - 1):
+                if slot == SUM_LAG + 4 * j + Y_LAG[j]:
+                    quantize_y(j, 0, GROUP)
+            if slot == LAST_FIRST_PAIR:
+                quantize_y(PANELS - 1, 0, HALF)
+            if slot == LAST_SECOND_PAIR:
+                quantize_y(PANELS - 1, HALF, GROUP)
+            for half in range(2, 8):
+                if slot == W_SLOTS[half - 2][1]:
+                    quantize_w(half)
+            for part in range(4):
+                if slot == A_QUANTIZE_SLOTS[part]:
+                    quantize_a(part)
+            if slot == W_SECOND_HALF_SLOT:
+                quantize_w(1)
+            if slot == VECTORS_SLOT:
+                vectors_onto_partitions()
+            for m in pair_behind(slot, Z_LAG - 1, UNITS):
+                quantize_z(m)
+
+            for m in pair_behind(slot, GAIN_LAG - 1, UNITS - 1):
+                apply_gain(m)
+            for engine, i, lo, hi in roundings:
                 if engine == "g":
-                    round_y(engine, j, pair, lo, hi)
+                    round_y(engine, i, lo, hi)
+
             for n in range(8):
-                if slot == A_SLOTS[n]:
+                if slot == A_TURN_SLOTS[n]:
                     turn_a(n)
-            for n in due(slot, SUM_LAG - 1, 32):
-                turn_kc(n // 4, n % 4, "tn" if slot < TAIL or n % 2 == 0 else "h")
-            for n in due(slot, SUM_LAG + 1 + TURN_LAG, 31):
-                if n % 2 == 1:
-                    turn_y(n // 4, (n % 4) // 2, "wt" if slot < KC_LAG + 33 or n % 4 == 1 else "kt")
-            for n in due(slot, -1, 32):
-                if n > 1:
-                    lift(n)
-            for n in due(slot, KC_LAG - 1, 32):
+            for n in range(BANKS):
+                if slot == n + SUM_LAG - (2 if n in EARLY_TURNS else 1):
+                    turn_kc(n, "turned" if slot < FREE_LIFT_BANKS or n % 5 in (0, 2) else "lifted")
+            for i in pair_behind(slot, TURN_LAG, 2 * PANELS - 1):
+                turn_y(i, "words" if slot < FREE_COUPLE_BANKS or i % 2 == 0 else "coupled")
+            for n in behind(slot, -1, BANKS):
+                lift(n)
+            for n in behind(slot, SCALE_LAG - 1, BANKS):
                 couple(n)
+
             if slot == 2:
                 reduce_angle(1)
-                quantize_w(0, 256, 512)
-            for n in due(slot, 0, 32):
+            for n in behind(slot, 0, BANKS):
                 count_turns(n)
-            for n in due(slot, SUM_LAG, 32):
-                add_control(n // 4, n % 4)
-            for n in due(slot, 1, 32):
-                if n > 1:
+            for n in behind(slot, SUM_LAG, BANKS):
+                add_control(n)
+            if slot > 2:
+                for n in behind(slot, 1, BANKS):
                     reduce_angle(n)
-            for n in due(slot, 2, 32):
-                if n % 2 == 1:
-                    cosine(n // 2)
-            for engine, j, pair, lo, hi in casts:
-                if engine != "g":
-                    round_y(engine, j, pair, lo, hi)
-            for n in due(slot, KC_LAG, 32):
-                scale_c(n)
-            for n in due(slot, SUM_LAG + 1 + TURN_LAG + UNLOAD_LAG, 31):
-                if n % 2 == 1:
-                    unload_y(n // 4, (n % 4) // 2)
-            if slot == SUM_LAG + 28 + LAST_LAG:
-                finish_last()
-            if slot == SUM_LAG + 28 + LAST_LAG + LAST_GAP:
-                finish_unload()
+
+            for m in pair_behind(slot, 2, UNITS):
+                cosine(m)
+            for engine, i, lo, hi in roundings:
+                if engine == "s":
+                    round_y(engine, i, lo, hi)
+            for n in behind(slot, SCALE_LAG, BANKS):
+                scale_by_c(n)
+            for i in pair_behind(slot, TURN_LAG, 2 * PANELS - 1):
+                unload_y(i)
+            if slot == LAST_ROUND:
+                round_and_turn_last_pair()
+            if slot == LAST_UNLOAD:
+                unload_last_pair()
             for n in range(8):
-                if slot == A_SLOTS[n] + 1:
+                if slot == A_TURN_SLOTS[n] + 1:
                     unload_a(n)
-            for when, engine, G, lo, hi, when_q in W_PLAN:
-                if slot == when and engine == "s":
-                    interleave_w(engine, G, lo, hi)
+            for half in range(2, 8):
+                if slot == W_SLOTS[half - 2][0]:
+                    interleave_w("s", half)

import math
from contextlib import ExitStack

import concourse.mybir as mybir
from concourse.masks import make_identity

S, D, F = 1024, 512, 2048
FLOPS = 2 * S * D * F + 2 * S * S * F

F32 = mybir.dt.float32
BF16 = mybir.dt.bfloat16
I32 = mybir.dt.int32
U32 = mybir.dt.uint32
U8 = mybir.dt.uint8
FP8X4 = mybir.dt.float8_e4m3fn_x4
ALU = mybir.AluOpType
ACT = mybir.ActivationFunctionType

P = 128
GROUP = 512
HALF = 256
BANKS = 32
UNITS = 16
PANELS = 8
PSUM_BUFS = {"lifted": 3, "coupled": 2, "turned": 2, "words": 1}

GAIN_LAG = 4
Z_LAG = 6
SCALE_LAG = 9
SUM_LAG = 16
ROUND_LAG = SUM_LAG + 1
TURN_LAG = ROUND_LAG + 2
Y_LAG = (12, 12, 12, 10, 8, 10, 11)
LAST_FIRST_PAIR, LAST_ROUND, LAST_UNLOAD, LAST_SECOND_PAIR = 54, 50, 53, 55
SLOTS = LAST_SECOND_PAIR + 1
FREE_LIFT_BANKS = 33
FREE_COUPLE_BANKS = SCALE_LAG + BANKS + 1
EARLY_TURNS = (19, 20, 21, 22, 23, 26, 27, 28, 29, 30, 31)

COUPLE_ORDER = ((0, 0), (1, 0), (0, 1), (1, 1), (2, 0), (3, 0), (2, 1), (3, 1))

A_TURN_SLOTS = (2, 2, 3, 5, 6, 6, 7, 7)
A_QUANTIZE_SLOTS = (6, 8, 10, 10)
W_SLOTS = ((3, 6), (5, 8), (10, 14), (11, 16), (15, 20), (19, 22))
W_SECOND_HALF_SLOT = 3
VECTORS_SLOT = 8

ROUND_ENGINE = "sssssssssshghgs"
SCALE_ON_VECTOR = (23, 24, 28)
UNLOAD_ON_VECTOR = 14


def tile_network_koopman_step_h3_kernel(tc, x, w, gain, a, c, u, b, out_0, out_1, out_2):
    nc = tc.nc
    with ExitStack() as ctx:
        keep = ctx.enter_context(tc.tile_pool(name="keep", bufs=1))
        work = ctx.enter_context(tc.tile_pool(name="work", bufs=2))
        psum = ctx.enter_context(tc.psum_pool(name="psum", bufs=2))
        ctx.enter_context(tc.manual_schedule())
        live = {}

        def bank(tag):
            return psum.tile([P, GROUP], F32, name=tag, tag=tag, bufs=PSUM_BUFS[tag])

        def quantize(codes, scales, grouped):
            nc.vector.quantize_mx(out=codes.bitcast(FP8X4), scales=scales, in_=grouped)

        def gpsimd_copy(out, in_):
            nc.gpsimd.tensor_scalar(out=out, in0=in_, scalar1=1.0, scalar2=1.0, op0=ALU.mult, op1=ALU.mult)

        copies = {"g": gpsimd_copy, "s": nc.scalar.copy, "v": nc.vector.tensor_copy}

        x_raw = [keep.tile([P, 2, D], BF16, name="x_raw%d" % piece) for piece in range(4)]
        w_raw = [keep.tile([P, 4, GROUP], BF16, name="w_raw%d" % og) for og in range(4)]
        a_raw = [keep.tile([P, 4, S], BF16, name="a_raw%d" % h) for h in range(2)]
        gain_raw = keep.tile([P, 2, 4], BF16)
        rows = keep.tile([P, P], BF16)
        b_all = keep.tile([P, F], BF16)
        ident = keep.tile([P, P], F32)
        warm = keep.tile([P, 1], F32)

        def load_x(piece):
            g, pair = divmod(piece, 2)
            sites = x[GROUP * g : GROUP * (g + 1), :].rearrange("(p t) d -> p t d", t=4)
            nc.sync.dma_start(out=x_raw[piece][:], in_=sites[:, 2 * pair : 2 * pair + 2, :])

        def load_w(og, lo, hi):
            cols = slice(GROUP * og + lo, GROUP * og + hi)
            nc.sync.dma_start(out=w_raw[og][:, :, lo:hi], in_=w[:, cols].rearrange("(p t) f -> p t f", t=4))

        def load_a(h):
            nc.sync.dma_start(out=a_raw[h][:], in_=a[GROUP * h : GROUP * (h + 1), :].rearrange("(s p) k -> p s k", p=P))

        nc.vector.memset(rows[:], 0.0)
        make_identity(nc, ident[:])
        nc.scalar.activation(out=warm[:], in_=rows[:, 0:1], func=ACT.Sin)
        load_x(0)
        nc.sync.dma_start(out=gain_raw[:], in_=gain.rearrange("(g p t) -> p g t", g=2, t=4))
        load_x(1)
        load_w(0, 0, HALF)
        load_x(2)
        load_x(3)
        load_w(0, HALF, GROUP)
        load_a(0)
        load_w(1, 0, GROUP)
        load_w(2, 0, GROUP)
        load_a(1)
        nc.sync.dma_start(out=rows[0:16, :], in_=c.rearrange("(r p) -> r p", p=P))
        nc.sync.dma_start(out=rows[16:24, :], in_=u.rearrange("(r p) -> r p", p=P))
        load_w(3, 0, GROUP)
        nc.sync.dma_start(out=b_all[:], in_=b.partition_broadcast(P))

        gain_all = keep.tile([P, 2, 4 * HALF], F32)
        for g in range(2):
            nc.vector.tensor_copy(
                out=gain_all[:, g, :].rearrange("p (f t) -> p f t", t=4),
                in_=gain_raw[:, g : g + 1, :].to_broadcast([P, HALF, 4]),
            )

        x_codes = keep.tile([P, 2, GROUP], U32, align_bytes=64)
        x_scales = keep.tile([P, 2, GROUP], U8, align_bytes=64)
        w_codes = keep.tile([P, F], U32, align_bytes=64)
        w_scales = keep.tile([P, F], U8, align_bytes=64)
        a_codes = keep.tile([P, 2, S], U32, align_bytes=64)
        a_scales = keep.tile([P, 2, S], U8, align_bytes=64)
        z_codes = keep.tile([P, UNITS * HALF], U32, align_bytes=64)
        z_scales = keep.tile([P, UNITS * HALF], U8, align_bytes=64)
        y_scales = keep.tile([P, 4, S], U8, align_bytes=64)
        rows_f32 = keep.tile([P, P], F32)
        cu = keep.tile([P, 32], F32)
        x_grouped = [keep.tile([P, 4 * GROUP], BF16, name="x_grouped%d" % g, align_bytes=64) for g in range(2)]

        def turn_words(ps, source):
            view = ps[:].rearrange("p (s e m) -> p s e m", s=2, e=2)
            for s in range(2):
                for e in range(2):
                    nc.tensor.transpose(view[:, s, e, :], source(s, e), ident[:])

        def unload_words(engine, grouped, pair, ps):
            words = grouped[:].bitcast(F32)[:, GROUP * pair : GROUP * (pair + 1)]
            copies[engine](
                out=words.rearrange("p (s m e) -> p s m e", s=2, e=2), in_=ps[:].rearrange("p (s e m) -> p s m e", s=2, e=2)
            )

        def turn_x(piece):
            ps = bank("turned" if piece < 2 else "coupled")
            words = x_raw[piece][:].bitcast(F32)
            turn_words(ps, lambda s, e: words[:, s, e:256:2])
            unload_words("s", x_grouped[piece // 2], piece % 2, ps)

        def quantize_x(piece):
            g, pair = divmod(piece, 2)
            cols = slice(HALF * pair, HALF * (pair + 1))
            quantize(x_codes[:, g, cols], x_scales[:, g, cols], x_grouped[g][:, 4 * HALF * pair : 4 * HALF * (pair + 1)])

        def turn_a(n):
            h, g, pair = n // 4, (n // 2) % 2, n % 2
            second_of_slot = n > 0 and A_TURN_SLOTS[n] == A_TURN_SLOTS[n - 1]
            live["a_words", n] = bank("coupled" if second_of_slot else "turned")
            words = a_raw[h][:].bitcast(F32)
            turn_words(live["a_words", n], lambda s, e: words[:, 2 * pair + s, 256 * g + e : 256 * (g + 1) : 2])

        def unload_a(n):
            if n % 2 == 0:
                live["a_grouped", n // 2] = work.tile([P, 4 * GROUP], BF16, name="a_grouped", align_bytes=64)
            unload_words("s", live["a_grouped", n // 2], n % 2, live["a_words", n])

        def quantize_a(part):
            h, g = divmod(part, 2)
            cols = slice(GROUP * h, GROUP * (h + 1))
            quantize(a_codes[:, g, cols], a_scales[:, g, cols], live["a_grouped", part][:])

        def interleave_w(engine, half):
            og, lo = half // 2, HALF * (half % 2)
            live["w_grouped", half] = work.tile([P, 4 * HALF], BF16, name="w_grouped", align_bytes=64)
            copies[engine](
                out=live["w_grouped", half][:].rearrange("p (f i t) -> p f t i", i=4, t=4),
                in_=w_raw[og][:, :, lo : lo + HALF].rearrange("p t (f i) -> p f t i", i=4),
            )

        def quantize_w(half):
            cols = slice(HALF * half, HALF * (half + 1))
            quantize(w_codes[:, cols], w_scales[:, cols], live["w_grouped", half][:])

        def vectors_onto_partitions():
            nc.scalar.copy(out=rows_f32[:], in_=rows[:])
            ps = bank("words")
            nc.tensor.transpose(ps[:, 0:P], rows_f32[:], ident[:])
            nc.scalar.copy(out=cu[:], in_=ps[:, 0:32])

        def lift(n):
            half, g, pair = n // 4, (n // 2) % 2, n % 2
            live["h", n] = bank("lifted")
            w_cols = slice(HALF * half, HALF * (half + 1))
            for e in range(2):
                x_cols = slice(P * (2 * pair + e), P * (2 * pair + e + 1))
                nc.tensor.matmul_mx(
                    out=live["h", n][:, HALF * e : HALF * (e + 1)],
                    lhsT=x_codes[:, g, x_cols].bitcast(FP8X4),
                    lhsT_scale=x_scales[:, g, x_cols],
                    rhs=w_codes[:, w_cols].bitcast(FP8X4),
                    rhs_scale=w_scales[:, w_cols],
                    start=True,
                    stop=True,
                )

        def h_pairs(n):
            return live["h", n][:].rearrange("p (e f) -> p f e", e=2)

        def count_turns(n):
            live["turns", n] = work.tile([P, HALF, 2], I32, name="turns", bufs=3)
            nc.vector.tensor_scalar(
                out=live["turns", n][:], in0=h_pairs(n), scalar1=1.0 / (2.0 * math.pi), scalar2=0.25, op0=ALU.mult, op1=ALU.add
            )

        def reduce_angle(n):
            if n % 2 == 0:
                live["angle", n // 2] = work.tile([P, 2, HALF, 2], F32, name="angle")
            nc.vector.scalar_tensor_tensor(
                out=live["angle", n // 2][:, n % 2],
                in0=live["turns", n][:],
                scalar=-2.0 * math.pi,
                in1=h_pairs(n),
                op0=ALU.mult,
                op1=ALU.add,
            )

        def cosine(m):
            live["cos", m] = work.tile([P, 4 * HALF], F32, name="cos", bufs=3)
            nc.scalar.activation(
                out=live["cos", m][:].rearrange("p (f pair e) -> p f pair e", pair=2, e=2),
                in_=live["angle", m][:].rearrange("p pair f e -> p f pair e"),
                func=ACT.Sin,
                bias=math.pi / 2.0,
            )

        def apply_gain(m):
            last = m == UNITS - 1
            live["z", m] = work.tile([P, 4 * HALF], BF16, name="z_last" if last else "z", bufs=1, align_bytes=64)
            engine = nc.vector if last else nc.gpsimd
            engine.tensor_tensor(out=live["z", m][:], in0=live["cos", m][:], in1=gain_all[:, m % 2, :], op=ALU.mult)

        def quantize_z(m):
            cols = slice(HALF * m, HALF * (m + 1))
            quantize(z_codes[:, cols], z_scales[:, cols], live["z", m][:])

        def couple(n):
            q, h = COUPLE_ORDER[n % 8]
            tile = 4 * (n // 8) + q
            live["kt", n] = bank("coupled")
            a_cols = slice(GROUP * h, GROUP * (h + 1))
            for g in range(2):
                first = HALF * (2 * (tile // 2) + g) + P * (tile % 2)
                nc.tensor.matmul_mx(
                    out=live["kt", n][:],
                    lhsT=z_codes[:, first : first + P].bitcast(FP8X4),
                    lhsT_scale=z_scales[:, first : first + P],
                    rhs=a_codes[:, g, a_cols].bitcast(FP8X4),
                    rhs_scale=a_scales[:, g, a_cols],
                    start=(g == 0),
                    stop=(g == 1),
                )

        def scale_by_c(n):
            q, h = COUPLE_ORDER[n % 8]
            j, tile = 2 * (n // 8) + h, 4 * (n // 8) + q
            if q == 0:
                live["kc", j] = work.tile([P, 4, GROUP], F32, name="kc", bufs=3)
            dst, c_col = live["kc", j][:, q, :], cu[:, tile : tile + 1]
            if n in SCALE_ON_VECTOR:
                nc.vector.tensor_scalar(out=dst, in0=live["kt", n][:], scalar1=c_col, scalar2=None, op0=ALU.mult)
            else:
                nc.scalar.activation(out=dst, in_=live["kt", n][:], func=ACT.Copy, scale=c_col)

        def turn_kc(n, tag):
            j, s = divmod(n, 4)
            live["kc_turned", n] = bank(tag)
            for q in range(4):
                nc.tensor.transpose(live["kc_turned", n][:, P * q : P * (q + 1)], live["kc", j][:, q, P * s : P * (s + 1)], ident[:])

        def add_control(n):
            og, site_tile = divmod(n, 8)
            if n % 2 == 0:
                live["y", n // 2] = work.tile([P, 2, GROUP], F32, name="y", bufs=4)
            y = live["y", n // 2]
            cols = slice(GROUP * og, GROUP * (og + 1))
            nc.vector.scalar_tensor_tensor(
                out=y[:, n % 2, :],
                in0=b_all[:, cols],
                scalar=cu[:, 16 + site_tile : 17 + site_tile],
                in1=live["kc_turned", n][:],
                op0=ALU.mult,
                op1=ALU.add,
            )
            if n >= BANKS - 2:
                nc.sync.dma_start(out=out_0[P * site_tile : P * (site_tile + 1), cols], in_=y[:, n % 2, :])
            elif n % 2 == 1:
                sites = slice(P * (site_tile - 1), P * (site_tile + 1))
                nc.sync.dma_start(out=out_0[sites, cols].rearrange("(s p) f -> p s f", p=P), in_=y[:])

        def round_y(engine, i, lo, hi):
            if ("y_bf16", i) not in live:
                live["y_bf16", i] = work.tile([P, 2 * GROUP], BF16, name="y_bf16", bufs=3)
            dst = live["y_bf16", i][:].rearrange("p (e q v) -> p e q v", e=2, v=2)
            src = live["y", i][:].rearrange("p s (q e v) -> p e (s q) v", e=2, v=2)
            copies[engine](out=dst[:, :, lo:hi, :], in_=src[:, :, lo:hi, :])

        def turn_y(i, tag):
            live["y_words", i] = bank(tag)
            words = live["y_bf16", i][:].bitcast(F32)
            turn_words(live["y_words", i], lambda s, e: words[:, 256 * e + P * s : 256 * e + P * (s + 1)])

        def unload_y(i):
            if i % 2 == 0:
                live["y_grouped", i // 2] = work.tile([P, 4 * GROUP], BF16, name="y_grouped", align_bytes=64)
            unload_words("v" if i == UNLOAD_ON_VECTOR else "s", live["y_grouped", i // 2], i % 2, live["y_words", i])

        def round_and_turn_last_pair():
            for s in range(2):
                live["last_bf16", s] = work.tile([P, GROUP], BF16, name="last_bf16")
                copies["sv"[s]](
                    out=live["last_bf16", s][:].rearrange("p (e q v) -> p e q v", e=2, v=2),
                    in_=live["y", 2 * PANELS - 1][:, s, :].rearrange("p (q e v) -> p e q v", e=2, v=2),
                )
            for s in range(2):
                live["last_words", s] = bank("coupled")
                words = live["last_bf16", s][:].bitcast(F32)
                for e in range(2):
                    nc.tensor.transpose(live["last_words", s][:, P * e : P * (e + 1)], words[:, P * e : P * (e + 1)], ident[:])

        def unload_last_pair():
            for s in range(2):
                words = live["y_grouped", PANELS - 1][:].bitcast(F32)[:, 256 * (2 + s) : 256 * (3 + s)]
                copies["sv"[s]](
                    out=words.rearrange("p (m e) -> p m e", e=2),
                    in_=live["last_words", s][:, 0:256].rearrange("p (e m) -> p m e", e=2),
                )

        def quantize_y(j, lo, hi):
            og, h = divmod(j, 2)
            very_last = j == PANELS - 1 and hi == GROUP
            codes = work.tile([P, hi - lo], U32, name="y_codes", bufs=4, align_bytes=64)
            sites = slice(GROUP * h + lo, GROUP * h + hi)
            quantize(codes[:], y_scales[:, og, sites], live["y_grouped", j][:, 4 * lo : 4 * hi])
            queue = nc.scalar if very_last else nc.sync
            queue.dma_start(out=out_1[og, :, sites, :].rearrange("p m t -> p (m t)").bitcast(I32), in_=codes[:].bitcast(I32))
            if h == 1 and hi == GROUP:
                for quad in range(4):
                    queue = nc.scalar if very_last and quad % 2 == 1 else nc.sync
                    queue.dma_start(
                        out=out_2[og, 4 * quad : 4 * quad + 4, :].bitcast(I32),
                        in_=y_scales[32 * quad : 32 * quad + 4, og, :].bitcast(I32),
                    )

        def behind(slot, lag, count):
            return [slot - lag] if 0 <= slot - lag < count else []

        def pair_behind(slot, lag, count):
            return [n // 2 for n in behind(slot, lag, 2 * count) if n % 2 == 1]

        for piece in range(3):
            turn_x(piece)
        interleave_w("v", 0)
        quantize_x(0)
        quantize_w(0)
        lift(0)
        quantize_x(1)
        lift(1)
        turn_x(3)
        interleave_w("s", 1)
        count_turns(0)
        quantize_x(2)
        lift(2)
        count_turns(1)
        reduce_angle(0)
        quantize_x(3)

        for slot in range(2, SLOTS):
            roundings = []
            for i in pair_behind(slot, ROUND_LAG, 2 * PANELS - 1):
                if ROUND_ENGINE[i] == "h":
                    roundings.extend([("g", i, 0, P), ("s", i, P, 2 * P)])
                else:
                    roundings.append((ROUND_ENGINE[i], i, 0, 2 * P))

            if slot == 2 * (UNITS - 1) + GAIN_LAG:
                apply_gain(UNITS - 1)
            for j in range(PANELS - 1):
                if slot == SUM_LAG + 4 * j + Y_LAG[j]:
                    quantize_y(j, 0, GROUP)
            if slot == LAST_FIRST_PAIR:
                quantize_y(PANELS - 1, 0, HALF)
            if slot == LAST_SECOND_PAIR:
                quantize_y(PANELS - 1, HALF, GROUP)
            for half in range(2, 8):
                if slot == W_SLOTS[half - 2][1]:
                    quantize_w(half)
            for part in range(4):
                if slot == A_QUANTIZE_SLOTS[part]:
                    quantize_a(part)
            if slot == W_SECOND_HALF_SLOT:
                quantize_w(1)
            if slot == VECTORS_SLOT:
                vectors_onto_partitions()
            for m in pair_behind(slot, Z_LAG - 1, UNITS):
                quantize_z(m)

            for m in pair_behind(slot, GAIN_LAG - 1, UNITS - 1):
                apply_gain(m)
            for engine, i, lo, hi in roundings:
                if engine == "g":
                    round_y(engine, i, lo, hi)

            for n in range(8):
                if slot == A_TURN_SLOTS[n]:
                    turn_a(n)
            for n in range(BANKS):
                if slot == n + SUM_LAG - (2 if n in EARLY_TURNS else 1):
                    turn_kc(n, "turned" if slot < FREE_LIFT_BANKS or n % 5 in (0, 2) else "lifted")
            for i in pair_behind(slot, TURN_LAG, 2 * PANELS - 1):
                turn_y(i, "words" if slot < FREE_COUPLE_BANKS or i % 2 == 0 else "coupled")
            for n in behind(slot, -1, BANKS):
                lift(n)
            for n in behind(slot, SCALE_LAG - 1, BANKS):
                couple(n)

            if slot == 2:
                reduce_angle(1)
            for n in behind(slot, 0, BANKS):
                count_turns(n)
            for n in behind(slot, SUM_LAG, BANKS):
                add_control(n)
            if slot > 2:
                for n in behind(slot, 1, BANKS):
                    reduce_angle(n)

            for m in pair_behind(slot, 2, UNITS):
                cosine(m)
            for engine, i, lo, hi in roundings:
                if engine == "s":
                    round_y(engine, i, lo, hi)
            for n in behind(slot, SCALE_LAG, BANKS):
                scale_by_c(n)
            for i in pair_behind(slot, TURN_LAG, 2 * PANELS - 1):
                unload_y(i)
            if slot == LAST_ROUND:
                round_and_turn_last_pair()
            if slot == LAST_UNLOAD:
                unload_last_pair()
            for n in range(8):
                if slot == A_TURN_SLOTS[n] + 1:
                    unload_a(n)
            for half in range(2, 8):
                if slot == W_SLOTS[half - 2][0]:
                    interleave_w("s", half)
